import numpy as np
import ml_dtypes


def mxq(x, axis, fmt="e4m3"):
    dtype, down = {"e4m3": (ml_dtypes.float8_e4m3fn, 7), "e5m2": (ml_dtypes.float8_e5m2, 14)}[fmt]
    v = np.moveaxis(np.asarray(x, np.float32).astype(ml_dtypes.bfloat16).astype(np.float64), axis, -1)
    blocks = v.reshape(v.shape[:-1] + (-1, 32))
    amax = np.abs(blocks).max(-1, keepdims=True)
    byte = np.maximum(np.where(amax > 0, np.frexp(amax)[1] - 1 + 127, 0) - down, 1)
    scale = np.exp2(byte - 127.0)
    codes = (blocks / scale).astype(np.float32).astype(dtype).astype(np.float64)
    return np.moveaxis((codes * scale).reshape(v.shape), -1, axis)


WIDE = False


def mx_kscale(k):
    if not WIDE:
        return np.ones(k)
    levels = np.array([10, -10, 5, -5, 0])
    if k % 512:
        return np.exp2(np.random.permutation(np.resize(levels, k // 32))).repeat(32)
    a = np.empty((k // 512, 16))
    for p in range(k // 512):
        a[p, :8] = np.random.permutation(np.resize(levels, 8))
        for g in range(8):
            far = levels[np.abs(levels - a[p, g]) >= 10]
            a[p, g + 8] = far[np.random.randint(len(far))]
    return np.exp2(a.ravel()).repeat(32)


BF16 = ml_dtypes.bfloat16


def bf(x):
    return np.asarray(x, np.float32).astype(BF16)


def f64(x):
    return np.asarray(x).astype(np.float64)


E2M1 = np.array([0.0, 0.5, 1.0, 1.5, 2.0, 3.0, 4.0, 6.0, -0.0, -0.5, -1.0, -1.5, -2.0, -3.0, -4.0, -6.0])


def pack_weight(w, fmt):
    k, n = w.shape
    w = f64(bf(w)).reshape(k // 32, 32, n)
    amax = np.abs(w).max(1)
    if fmt == "e4m3":
        byte = np.frexp(amax)[1] - 1 + 127 - 7
    else:
        mant, ex = np.frexp(amax / 6.0)
        byte = np.where(mant > 0.5, ex, ex - 1) + 127
    byte = np.clip(np.where(amax > 0, byte, 1), 1, 254)
    scaled = (w * np.exp2(127.0 - byte)[:, None, :]).reshape(k, n).astype(np.float32)
    by_word = np.ascontiguousarray(scaled.reshape(k // 512, 128, 4, n).transpose(0, 1, 3, 2))
    if fmt == "e4m3":
        words = by_word.astype(ml_dtypes.float8_e4m3fn).view(np.uint8)
    else:
        c = by_word.astype(ml_dtypes.float4_e2m1fn).view(np.uint8) & 0xF
        words = c[..., 0::2] | (c[..., 1::2] << 4)
    return np.ascontiguousarray(words), np.ascontiguousarray(byte.astype(np.uint8).reshape(k // 512, 16, n))


def unpack_weight(words, scales, fmt):
    g, p, n, _ = words.shape
    if fmt == "e4m3":
        vals = np.ascontiguousarray(words).view(ml_dtypes.float8_e4m3fn).astype(np.float64)
    else:
        nib = np.empty((g, p, n, 4), np.uint8)
        nib[..., 0::2] = words & 0xF
        nib[..., 1::2] = words >> 4
        vals = E2M1[nib]
    vals = vals * np.repeat(np.exp2(scales.astype(np.float64) - 127.0), 8, axis=1)[..., None]
    return vals.transpose(0, 1, 3, 2).reshape(g * 512, n)
def pack4(w):
    words, scales = pack_weight(w, "e2m1")
    return words.reshape(words.shape[0], 128, -1), scales


def unpack4(words, scales):
    return unpack_weight(words.reshape(words.shape[0], 128, -1, 2), scales, "e2m1")


def planes(Y):
    n, m = Y.shape
    b = f64(bf(Y)).reshape(n // 32, 32, m)
    amax = np.abs(b).max(1)
    byte = np.clip(np.where(amax > 0, np.frexp(amax)[1] - 1 + 127 - 7, 1), 1, 254)
    codes = (b * np.exp2(127.0 - byte)[:, None, :]).reshape(n, m).astype(np.float32).astype(ml_dtypes.float8_e4m3fn).view(np.uint8)
    words = codes.reshape(n // 512, 128, 4, m).transpose(0, 1, 3, 2)
    return np.ascontiguousarray(words), np.ascontiguousarray(byte.astype(np.uint8).reshape(n // 512, 16, m))


D, S = 1024, 1536

SLOPE = 0.25

def setup_inputs():
    s = mx_kscale(D)
    t = mx_kscale(D)
    links = np.random.randn(D, D) * D ** -0.25
    left_words, left_scales = pack_weight((links * s[None, :]).T, "e4m3")
    right_words, right_scales = pack4(links / s[:, None])
    node_weight = 0.3 * np.exp(0.3 * np.random.randn(D))
    strength = np.exp(0.8 * np.random.randn(S))
    seeds = np.random.randn(D, S) / np.sqrt(D) * strength[None, :]
    threshold = 0.4 * np.random.randn(S)
    return {
        "left_words": left_words, "left_scales": left_scales,
        "right_words": right_words, "right_scales": right_scales,
        "node_weight": bf(node_weight * t),
        "seeds": bf(seeds / t[:, None]),
        "threshold": bf(threshold),
    }

def reference(left_words, left_scales, right_words, right_scales, node_weight, seeds, threshold):
    P = unpack_weight(left_words, left_scales, "e4m3")
    Q = unpack4(right_words, right_scales)
    E = P.T @ Q
    H = E * E * E * f64(node_weight)
    Z = mxq(H, 1, "e4m3") @ mxq(f64(seeds), 0, "e4m3")
    d = Z - f64(threshold)
    y = np.maximum(d, SLOPE * d)
    words, scales = planes(y.T)
    return y, words, scales

@@ -1,0 +1,360 @@
+from contextlib import ExitStack
+
+import concourse.mybir as mybir
+from concourse.masks import make_identity
+
+D, S = 1024, 1536
+SLOPE = 0.25
+FLOPS = 2 * D * D * D + 2 * D * D * S
+
+F32 = mybir.dt.float32
+BF16 = mybir.dt.bfloat16
+I32 = mybir.dt.int32
+U32 = mybir.dt.uint32
+U8 = mybir.dt.uint8
+FP8X4 = mybir.dt.float8_e4m3fn_x4
+FP4X4 = mybir.dt.float4_e2m1fn_x4
+ALU = mybir.AluOpType
+ACT = mybir.ActivationFunctionType
+
+P = 128
+PACK = 4
+W = 512
+NG = D // W
+SG = S // W
+
+
+def tile_cubed_walk_seed_scores_h2_kernel(
+    tc, left_words, left_scales, right_words, right_scales, node_weight, seeds, threshold, out_0, out_1, out_2
+):
+    nc = tc.nc
+    with ExitStack() as ctx:
+        keep = ctx.enter_context(tc.tile_pool(name="keep", bufs=1))
+        work = ctx.enter_context(tc.tile_pool(name="work", bufs=2))
+        psum = ctx.enter_context(tc.psum_pool(name="psum", bufs=8))
+        ctx.enter_context(tc.manual_schedule())
+
+        def kept(name, shape, dtype):
+            return keep.tile(shape, dtype, name=name, align_bytes=64)
+
+        q_raw = [kept("q_raw%d" % g, [P, NG, 2 * W], U8) for g in range(NG)]
+        qs_raw = kept("qs_raw", [P, NG, D], U8)
+        ps = kept("ps", [P, NG, D], U8)
+        p_words = [kept("p_words%d" % h, [P, NG, W], U32) for h in range(NG)]
+        q_words = [kept("q_words%d" % g, [P, NG, 2 * W], U8) for g in range(NG)]
+        qs = [kept("qs%d" % g, [P, NG, W], U8) for g in range(NG)]
+        w_rows = kept("w_rows", [P, NG, P], BF16)
+        ident_h = kept("ident_h", [P, P], BF16)
+        w_col = kept("w_col", [P, NG, PACK], F32)
+        t_raw = kept("t_raw", [P, SG, PACK], BF16)
+        t_col = kept("t_col", [P, SG, PACK], F32)
+        t_bias = kept("t_bias", [P, SG, PACK], F32)
+        ident = kept("ident", [P, P], F32)
+        warm = kept("warm", [P, 1], F32)
+        s_first = [kept("s_first%d" % g, [P, PACK, W], BF16) for g in range(NG)]
+        s_rest = [kept("s_rest%d" % g, [P, PACK, S - W], BF16) for g in range(NG)]
+        s_codes = {}
+        s_scales = {}
+        s_grouped = {}
+        for sg in range(SG):
+            for g in range(NG):
+                s_codes[g, sg] = kept("s_codes%d%d" % (g, sg), [P, W], U32)
+                s_scales[g, sg] = kept("s_scales%d%d" % (g, sg), [P, W], U8)
+        h_codes = {}
+        h_scales = {}
+        for h in range(NG):
+            for g in range(NG):
+                h_codes[h, g] = kept("h_codes%d%d" % (h, g), [P, W], U32)
+                h_scales[h, g] = kept("h_scales%d%d" % (h, g), [P, W], U8)
+        y_codes = {}
+        for h in range(NG):
+            for sg in range(SG):
+                y_codes[h, sg] = kept("y_codes%d%d" % (h, sg), [P, W], U32)
+        y_scales = [kept("y_scales%d" % h, [P, SG, W], U8) for h in range(NG)]
+
+        nc.gpsimd.memset(ps[:].rearrange("p g n -> p (g n)").bitcast(I32), 0)
+        nc.vector.memset(qs_raw[:].rearrange("p g n -> p (g n)").bitcast(I32), 0)
+        nc.vector.memset(w_rows[:], 0.0)
+        nc.vector.memset(warm[:], 0.0)
+        nc.scalar.activation(out=warm[:], in_=warm[:], func=ACT.Square)
+
+        def load_p(h, queue):
+            src = left_words.rearrange("g p n t -> p g (n t)")[:, :, h * W * PACK : (h + 1) * W * PACK]
+            queue.dma_start(out=p_words[h][:].bitcast(I32), in_=src.bitcast(I32))
+
+        def load_scales(plane, src, q, queue):
+            rows = src.rearrange("g r n -> r g n")[4 * q : 4 * q + 4]
+            queue.dma_start(out=plane[32 * q : 32 * q + 4].bitcast(I32), in_=rows.bitcast(I32))
+
+        def load_seeds(g, c0, c1, t, queue):
+            src = seeds[g * W : (g + 1) * W, c0:c1].rearrange("(b t r) s -> t b r s", t=PACK, r=8)
+            queue.dma_start(out=(s_first if c0 == 0 else s_rest)[g][:, t, :], in_=src[t])
+
+        def load_q(g, queue):
+            src = right_words.rearrange("c p n -> p c n")[:, :, g * 2 * W : (g + 1) * 2 * W]
+            queue.dma_start(out=q_raw[g][:].bitcast(I32), in_=src.bitcast(I32))
+
+
+        def load_w(queue):
+            src = node_weight.rearrange("(b t r) -> t b r", t=PACK, r=8)
+            queue.dma_start(out=w_rows[:PACK].rearrange("t g (b r) -> t (g b) r", r=8), in_=src)
+
+        def load_t(queue):
+            queue.dma_start(out=t_raw[:], in_=threshold.rearrange("(g p t) -> p g t", p=P, t=PACK))
+
+        def permute_q(g):
+            nc.vector.tensor_copy(
+                out=q_words[g][:].bitcast(I32).rearrange("p c (t b r) -> p c t b r", t=PACK, r=4),
+                in_=q_raw[g][:].bitcast(I32).rearrange("p c (b t r) -> p c t b r", t=PACK, r=4),
+            )
+            nc.vector.tensor_copy(
+                out=qs[g][:].bitcast(I32).rearrange("p c (t b r) -> p c t b r", t=PACK, r=2),
+                in_=qs_raw[:, :, g * W : (g + 1) * W].bitcast(I32).rearrange("p c (b t r) -> p c t b r", t=PACK, r=2),
+            )
+
+        def weights():
+            bank = psum.tile([P, NG, P], BF16, name="bank")
+            for g in range(NG):
+                nc.tensor.transpose(bank[:, g, :], w_rows[:, g, :], ident_h[:])
+            nc.vector.tensor_copy(out=w_col[:], in_=bank[:, :, :PACK])
+
+        def interleave(dst, src, engine):
+            if engine == "S":
+                nc.scalar.copy(out=dst, in_=src)
+            elif engine == "V":
+                nc.vector.tensor_copy(out=dst, in_=src)
+            else:
+                nc.gpsimd.tensor_scalar(out=dst, in0=src, scalar1=1.0, scalar2=1.0, op0=ALU.mult, op1=ALU.mult)
+
+        def grouped_tile(engine):
+            return work.tile([P, W, PACK], BF16, name="grouped" + engine, bufs=1 if engine == "G" else 2, align_bytes=64)
+
+        def seeds_group(g, sg, engine):
+            grouped = grouped_tile(engine)
+            s_grouped[g, sg] = grouped
+            dst = grouped[:].rearrange("p (t m) j -> p t m j", t=PACK)
+            src = (s_first[g][:] if sg == 0 else s_rest[g][:, :, (sg - 1) * W : sg * W]).rearrange("p j (m t) -> p t m j", t=PACK)
+            interleave(dst, src, engine)
+
+        def quantize(codes, scales, grouped):
+            nc.vector.quantize_mx(out=codes.bitcast(FP8X4), scales=scales, in_=grouped[:].rearrange("p m t -> p (m t)"))
+
+        def seeds_quant(g, sg):
+            quantize(s_codes[g, sg][:], s_scales[g, sg][:], s_grouped[g, sg])
+
+        rows = {}
+        grouped_of = {}
+
+        def walk(h, g, t):
+            if t == 0:
+                rows["A", h, g] = work.tile([P, PACK, W], BF16, name="hb", bufs=3, align_bytes=64)
+            hb = rows["A", h, g]
+            if True:
+                bank = psum.tile([P, W], F32, name="bank")
+                for c in range(NG):
+                    nc.tensor.matmul_mx(
+                        out=bank[:],
+                        lhsT=q_words[g][:, c, t * 2 * P : (t + 1) * 2 * P].bitcast(FP4X4),
+                        lhsT_scale=qs[g][:, c, t * P : (t + 1) * P],
+                        rhs=p_words[h][:, c, :].bitcast(FP8X4),
+                        rhs_scale=ps[:, c, h * W : (h + 1) * W],
+                        start=(c == 0),
+                        stop=(c == NG - 1),
+                    )
+                sq = work.tile([P, W], F32, name="sq", bufs=4)
+                nc.scalar.activation(out=sq[:], in_=bank[:], func=ACT.Square)
+                nc.vector.scalar_tensor_tensor(
+                    out=hb[:, t, :], in0=bank[:], scalar=w_col[:, g, t : t + 1], in1=sq[:], op0=ALU.mult, op1=ALU.mult
+                )
+
+        def score(h, sg, t):
+            if t == 0:
+                rows["B", h, sg] = work.tile([P, PACK, W], F32, name="yt", bufs=3)
+            yt = rows["B", h, sg]
+            if True:
+                bank = psum.tile([P, W], F32, name="bank")
+                for c in range(NG):
+                    nc.tensor.matmul_mx(
+                        out=bank[:],
+                        lhsT=s_codes[c, sg][:, t * P : (t + 1) * P].bitcast(FP8X4),
+                        lhsT_scale=s_scales[c, sg][:, t * P : (t + 1) * P],
+                        rhs=h_codes[h, c][:].bitcast(FP8X4),
+                        rhs_scale=h_scales[h, c][:],
+                        start=(c == 0),
+                        stop=(c == NG - 1),
+                    )
+                low = work.tile([P, W], F32, name="sq", bufs=4)
+                nc.scalar.activation(
+                    out=low[:], in_=bank[:], func=ACT.Identity, scale=SLOPE, bias=t_bias[:, sg, t : t + 1]
+                )
+                nc.vector.scalar_tensor_tensor(
+                    out=yt[:, t, :], in0=bank[:], scalar=t_col[:, sg, t : t + 1], in1=low[:], op0=ALU.subtract, op1=ALU.max
+                )
+
+        def group(key, engine):
+            grouped = grouped_tile(engine)
+            grouped_of[key] = grouped
+            interleave(grouped[:], rows[key][:].rearrange("p t m -> p m t"), engine)
+
+        def quant(key):
+            kind, h, g = key
+            if kind == "A":
+                quantize(h_codes[h, g][:], h_scales[h, g][:], grouped_of[key])
+            else:
+                quantize(y_codes[h, g][:], y_scales[h][:, g, :], grouped_of[key])
+                dst = out_1[g].rearrange("p m t -> p (m t)")[:, h * W * PACK : (h + 1) * W * PACK]
+                nc.sync.dma_start(out=dst.bitcast(I32), in_=y_codes[h, g][:].bitcast(I32))
+                if g == SG - 1:
+                    for q in range(4):
+                        dst = out_2.rearrange("g r m -> r g m")[4 * q : 4 * q + 4, :, h * W : (h + 1) * W]
+                        nc.sync.dma_start(out=dst.bitcast(I32), in_=y_scales[h][32 * q : 32 * q + 4].bitcast(I32))
+
+        def turn(h, sg, mt, engine):
+            yt = rows["B", h, sg]
+            if True:
+                bank = psum.tile([P, PACK, P], F32, name="bank")
+                for t in range(PACK):
+                    nc.tensor.transpose(bank[:, t, :], yt[:, t, mt * P : (mt + 1) * P], ident[:])
+                y = work.tile([P, W], F32, name="y", bufs=8)
+                dst = y[:].rearrange("m (p t) -> m p t", t=PACK)
+                src = bank[:].rearrange("m t p -> m p t")
+                if engine == "V":
+                    nc.vector.tensor_copy(out=dst, in_=src)
+                else:
+                    nc.scalar.copy(out=dst, in_=src)
+                m0 = h * W + mt * P
+                nc.sync.dma_start(out=out_0[m0 : m0 + P, sg * W : (sg + 1) * W], in_=y[:])
+
+        load_seeds(1, 0, W, 0, nc.sync)
+        load_seeds(1, 0, W, 1, nc.sync)
+        load_seeds(1, 0, W, 2, nc.sync)
+        load_seeds(1, 0, W, 3, nc.sync)
+        seeds_group(1, 0, "V")
+        load_seeds(0, 0, W, 0, nc.sync)
+        load_seeds(0, 0, W, 1, nc.sync)
+        load_seeds(0, 0, W, 2, nc.sync)
+        load_seeds(0, 0, W, 3, nc.sync)
+        load_t(nc.sync)
+        load_seeds(0, W, S, 0, nc.sync)
+        load_seeds(0, W, S, 1, nc.sync)
+        load_seeds(0, W, S, 2, nc.sync)
+        load_seeds(0, W, S, 3, nc.sync)
+        seeds_group(0, 0, "V")
+        load_w(nc.sync)
+        seeds_quant(1, 0)
+        load_scales(qs_raw, right_scales, 0, nc.sync)
+        load_scales(qs_raw, right_scales, 1, nc.sync)
+        load_scales(qs_raw, right_scales, 2, nc.sync)
+        load_scales(qs_raw, right_scales, 3, nc.sync)
+        seeds_quant(0, 0)
+        seeds_group(0, 1, "V")
+        load_q(0, nc.sync)
+        make_identity(nc, ident_h[:])
+        load_p(0, nc.sync)
+        permute_q(0)
+        seeds_quant(0, 1)
+        nc.vector.tensor_copy(out=t_col[:], in_=t_raw[:])
+        nc.vector.tensor_scalar_mul(out=t_bias[:], in0=t_raw[:], scalar1=-SLOPE)
+        load_scales(ps, left_scales, 0, nc.sync)
+        load_scales(ps, left_scales, 1, nc.sync)
+        load_scales(ps, left_scales, 2, nc.sync)
+        load_scales(ps, left_scales, 3, nc.sync)
+        load_q(1, nc.sync)
+        seeds_group(0, 2, "S")
+        load_seeds(1, W, S, 0, nc.sync)
+        load_seeds(1, W, S, 1, nc.sync)
+        load_seeds(1, W, S, 2, nc.sync)
+        load_seeds(1, W, S, 3, nc.sync)
+        permute_q(1)
+        weights()
+        seeds_quant(0, 2)
+        walk(0, 0, 0)
+        walk(0, 0, 1)
+        make_identity(nc, ident[:])
+        walk(0, 1, 0)
+        walk(0, 1, 1)
+        seeds_group(1, 2, "G")
+        walk(0, 1, 2)
+        walk(0, 1, 3)
+        walk(0, 0, 2)
+        walk(0, 0, 3)
+        group(("A", 0, 1), "V")
+        load_p(1, nc.sync)
+        walk(1, 1, 0)
+        walk(1, 1, 1)
+        group(("A", 0, 0), "S")
+        quant(("A", 0, 1))
+        quant(("A", 0, 0))
+        seeds_quant(1, 2)
+        walk(1, 0, 0)
+        walk(1, 0, 1)
+        seeds_group(1, 1, "G")
+        walk(1, 0, 2)
+        walk(1, 0, 3)
+        score(0, 0, 0)
+        score(0, 0, 1)
+        seeds_quant(1, 1)
+        score(0, 0, 2)
+        score(0, 0, 3)
+        group(("A", 1, 0), "G")
+        walk(1, 1, 2)
+        walk(1, 1, 3)
+        score(0, 1, 0)
+        score(0, 1, 1)
+        quant(("A", 1, 0))
+        score(0, 2, 0)
+        score(0, 2, 1)
+        group(("A", 1, 1), "G")
+        turn(0, 0, 0, "S")
+        turn(0, 0, 1, "S")
+        score(0, 2, 2)
+        score(0, 2, 3)
+        score(0, 1, 2)
+        score(0, 1, 3)
+        group(("B", 0, 0), "S")
+        quant(("A", 1, 1))
+        turn(0, 2, 0, "V")
+        turn(0, 2, 1, "V")
+        turn(0, 0, 2, "V")
+        turn(0, 0, 3, "V")
+        score(1, 1, 0)
+        score(1, 1, 1)
+        group(("B", 0, 1), "G")
+        turn(0, 1, 2, "S")
+        turn(0, 1, 3, "S")
+        quant(("B", 0, 1))
+        turn(0, 1, 0, "V")
+        turn(0, 1, 1, "V")
+        score(1, 1, 2)
+        score(1, 1, 3)
+        score(1, 0, 0)
+        score(1, 0, 1)
+        group(("B", 0, 2), "G")
+        turn(0, 2, 2, "S")
+        turn(0, 2, 3, "S")
+        quant(("B", 0, 0))
+        quant(("B", 0, 2))
+        group(("B", 1, 1), "G")
+        turn(1, 1, 2, "S")
+        turn(1, 1, 3, "V")
+        score(1, 0, 2)
+        score(1, 0, 3)
+        score(1, 2, 0)
+        score(1, 2, 1)
+        turn(1, 1, 0, "S")
+        turn(1, 1, 1, "S")
+        turn(1, 0, 2, "S")
+        turn(1, 0, 3, "V")
+        quant(("B", 1, 1))
+        score(1, 2, 2)
+        score(1, 2, 3)
+        turn(1, 0, 0, "S")
+        turn(1, 0, 1, "S")
+        group(("B", 1, 0), "V")
+        turn(1, 2, 0, "S")
+        turn(1, 2, 1, "S")
+        group(("B", 1, 2), "V")
+        turn(1, 2, 2, "S")
+        turn(1, 2, 3, "S")
+        quant(("B", 1, 0))
+        quant(("B", 1, 2))

@@ -72,10 +72,10 @@ def tile_cubed_walk_seed_scores_h2_kernel(
                 y_codes[h, sg] = kept("y_codes%d%d" % (h, sg), [P, W], U32)
         y_scales = [kept("y_scales%d" % h, [P, SG, W], U8) for h in range(NG)]
 
+        nc.vector.memset(warm[:], 0.0)
         nc.gpsimd.memset(ps[:].rearrange("p g n -> p (g n)").bitcast(I32), 0)
         nc.vector.memset(qs_raw[:].rearrange("p g n -> p (g n)").bitcast(I32), 0)
         nc.vector.memset(w_rows[:], 0.0)
-        nc.vector.memset(warm[:], 0.0)
         nc.scalar.activation(out=warm[:], in_=warm[:], func=ACT.Square)
 
         def load_p(h, queue):
@@ -194,7 +194,11 @@ def tile_cubed_walk_seed_scores_h2_kernel(
         def group(key, engine):
             grouped = grouped_tile(engine)
             grouped_of[key] = grouped
-            interleave(grouped[:], rows[key][:].rearrange("p t m -> p m t"), engine)
+            interleave(
+                grouped[:].rearrange("p (c i) t -> p c t i", i=4),
+                rows[key][:].rearrange("p t (c i) -> p c t i", i=4),
+                engine,
+            )
 
         def quant(key):
             kind, h, g = key
@@ -225,136 +229,136 @@ def tile_cubed_walk_seed_scores_h2_kernel(
                 m0 = h * W + mt * P
                 nc.sync.dma_start(out=out_0[m0 : m0 + P, sg * W : (sg + 1) * W], in_=y[:])
 
-        load_seeds(1, 0, W, 0, nc.sync)
-        load_seeds(1, 0, W, 1, nc.sync)
-        load_seeds(1, 0, W, 2, nc.sync)
-        load_seeds(1, 0, W, 3, nc.sync)
-        seeds_group(1, 0, "V")
-        load_seeds(0, 0, W, 0, nc.sync)
-        load_seeds(0, 0, W, 1, nc.sync)
-        load_seeds(0, 0, W, 2, nc.sync)
-        load_seeds(0, 0, W, 3, nc.sync)
-        load_t(nc.sync)
         load_seeds(0, W, S, 0, nc.sync)
         load_seeds(0, W, S, 1, nc.sync)
         load_seeds(0, W, S, 2, nc.sync)
         load_seeds(0, W, S, 3, nc.sync)
-        seeds_group(0, 0, "V")
-        load_w(nc.sync)
-        seeds_quant(1, 0)
+        load_q(0, nc.sync)
         load_scales(qs_raw, right_scales, 0, nc.sync)
         load_scales(qs_raw, right_scales, 1, nc.sync)
         load_scales(qs_raw, right_scales, 2, nc.sync)
         load_scales(qs_raw, right_scales, 3, nc.sync)
-        seeds_quant(0, 0)
-        seeds_group(0, 1, "V")
-        load_q(0, nc.sync)
-        make_identity(nc, ident_h[:])
-        load_p(0, nc.sync)
-        permute_q(0)
-        seeds_quant(0, 1)
-        nc.vector.tensor_copy(out=t_col[:], in_=t_raw[:])
-        nc.vector.tensor_scalar_mul(out=t_bias[:], in0=t_raw[:], scalar1=-SLOPE)
-        load_scales(ps, left_scales, 0, nc.sync)
-        load_scales(ps, left_scales, 1, nc.sync)
-        load_scales(ps, left_scales, 2, nc.sync)
-        load_scales(ps, left_scales, 3, nc.sync)
-        load_q(1, nc.sync)
-        seeds_group(0, 2, "S")
+        seeds_group(0, 2, "V")
         load_seeds(1, W, S, 0, nc.sync)
         load_seeds(1, W, S, 1, nc.sync)
         load_seeds(1, W, S, 2, nc.sync)
         load_seeds(1, W, S, 3, nc.sync)
-        permute_q(1)
-        weights()
+        seeds_group(0, 1, "S")
+        load_t(nc.sync)
+        load_w(nc.sync)
+        permute_q(0)
+        load_p(0, nc.sync)
+        make_identity(nc, ident_h[:])
+        load_scales(ps, left_scales, 0, nc.sync)
+        load_scales(ps, left_scales, 1, nc.sync)
+        load_scales(ps, left_scales, 2, nc.sync)
+        load_scales(ps, left_scales, 3, nc.sync)
         seeds_quant(0, 2)
+        load_q(1, nc.sync)
+        seeds_quant(0, 1)
+        seeds_group(1, 1, "S")
+        load_seeds(1, 0, W, 0, nc.sync)
+        load_seeds(1, 0, W, 1, nc.sync)
+        load_seeds(1, 0, W, 2, nc.sync)
+        load_seeds(1, 0, W, 3, nc.sync)
+        load_seeds(0, 0, W, 0, nc.sync)
+        load_seeds(0, 0, W, 1, nc.sync)
+        load_seeds(0, 0, W, 2, nc.sync)
+        load_seeds(0, 0, W, 3, nc.sync)
+        seeds_group(1, 2, "V")
+        nc.vector.tensor_copy(out=t_col[:], in_=t_raw[:])
+        nc.vector.tensor_scalar_mul(out=t_bias[:], in0=t_raw[:], scalar1=-SLOPE)
+        weights()
+        seeds_quant(1, 2)
+        permute_q(1)
+        seeds_quant(1, 1)
         walk(0, 0, 0)
         walk(0, 0, 1)
-        make_identity(nc, ident[:])
-        walk(0, 1, 0)
-        walk(0, 1, 1)
-        seeds_group(1, 2, "G")
-        walk(0, 1, 2)
-        walk(0, 1, 3)
         walk(0, 0, 2)
         walk(0, 0, 3)
-        group(("A", 0, 1), "V")
+        seeds_group(0, 0, "V")
+        walk(0, 1, 0)
+        walk(0, 1, 1)
+        seeds_group(1, 0, "V")
+        group(("A", 0, 0), "S")
+        walk(0, 1, 2)
+        walk(0, 1, 3)
         load_p(1, nc.sync)
+        seeds_quant(1, 0)
         walk(1, 1, 0)
         walk(1, 1, 1)
-        group(("A", 0, 0), "S")
-        quant(("A", 0, 1))
-        quant(("A", 0, 0))
-        seeds_quant(1, 2)
         walk(1, 0, 0)
         walk(1, 0, 1)
-        seeds_group(1, 1, "G")
-        walk(1, 0, 2)
-        walk(1, 0, 3)
-        score(0, 0, 0)
-        score(0, 0, 1)
-        seeds_quant(1, 1)
-        score(0, 0, 2)
-        score(0, 0, 3)
-        group(("A", 1, 0), "G")
+        quant(("A", 0, 0))
+        group(("A", 0, 1), "S")
+        seeds_quant(0, 0)
+        make_identity(nc, ident[:])
+        quant(("A", 0, 1))
         walk(1, 1, 2)
         walk(1, 1, 3)
-        score(0, 1, 0)
-        score(0, 1, 1)
-        quant(("A", 1, 0))
+        walk(1, 0, 2)
+        walk(1, 0, 3)
         score(0, 2, 0)
         score(0, 2, 1)
-        group(("A", 1, 1), "G")
-        turn(0, 0, 0, "S")
-        turn(0, 0, 1, "S")
+        score(0, 0, 0)
+        score(0, 0, 1)
         score(0, 2, 2)
         score(0, 2, 3)
-        score(0, 1, 2)
-        score(0, 1, 3)
-        group(("B", 0, 0), "S")
-        quant(("A", 1, 1))
-        turn(0, 2, 0, "V")
-        turn(0, 2, 1, "V")
-        turn(0, 0, 2, "V")
-        turn(0, 0, 3, "V")
-        score(1, 1, 0)
-        score(1, 1, 1)
-        group(("B", 0, 1), "G")
-        turn(0, 1, 2, "S")
-        turn(0, 1, 3, "S")
-        quant(("B", 0, 1))
-        turn(0, 1, 0, "V")
-        turn(0, 1, 1, "V")
-        score(1, 1, 2)
-        score(1, 1, 3)
-        score(1, 0, 0)
-        score(1, 0, 1)
-        group(("B", 0, 2), "G")
+        group(("A", 1, 0), "V")
+        score(0, 0, 2)
+        score(0, 0, 3)
+        score(0, 1, 0)
+        score(0, 1, 1)
         turn(0, 2, 2, "S")
         turn(0, 2, 3, "S")
+        score(0, 1, 2)
+        score(0, 1, 3)
+        quant(("A", 1, 0))
+        group(("A", 1, 1), "V")
+        group(("B", 0, 0), "V")
+        turn(0, 0, 2, "S")
+        turn(0, 0, 3, "S")
+        turn(0, 2, 0, "S")
+        turn(0, 2, 1, "S")
+        quant(("A", 1, 1))
+        turn(0, 0, 0, "S")
+        turn(0, 0, 1, "S")
         quant(("B", 0, 0))
-        quant(("B", 0, 2))
-        group(("B", 1, 1), "G")
-        turn(1, 1, 2, "S")
-        turn(1, 1, 3, "V")
+        group(("B", 0, 2), "S")
+        turn(0, 1, 2, "V")
+        turn(0, 1, 3, "S")
+        turn(0, 1, 0, "V")
+        turn(0, 1, 1, "S")
+        group(("B", 0, 1), "V")
+        score(1, 0, 0)
+        score(1, 0, 1)
+        quant(("B", 0, 1))
         score(1, 0, 2)
         score(1, 0, 3)
+        score(1, 1, 0)
+        score(1, 1, 1)
+        score(1, 1, 2)
+        score(1, 1, 3)
+        turn(1, 0, 2, "S")
+        turn(1, 0, 3, "S")
+        turn(1, 0, 0, "V")
+        turn(1, 0, 1, "S")
+        quant(("B", 0, 2))
         score(1, 2, 0)
         score(1, 2, 1)
-        turn(1, 1, 0, "S")
-        turn(1, 1, 1, "S")
-        turn(1, 0, 2, "S")
-        turn(1, 0, 3, "V")
-        quant(("B", 1, 1))
+        turn(1, 1, 2, "S")
+        turn(1, 1, 3, "V")
         score(1, 2, 2)
         score(1, 2, 3)
-        turn(1, 0, 0, "S")
-        turn(1, 0, 1, "S")
+        group(("B", 1, 1), "V")
+        turn(1, 1, 0, "S")
+        turn(1, 1, 1, "S")
         group(("B", 1, 0), "V")
-        turn(1, 2, 0, "S")
-        turn(1, 2, 1, "S")
-        group(("B", 1, 2), "V")
         turn(1, 2, 2, "S")
         turn(1, 2, 3, "S")
+        turn(1, 2, 0, "S")
+        turn(1, 2, 1, "V")
+        quant(("B", 1, 1))
         quant(("B", 1, 0))
+        group(("B", 1, 2), "S")
         quant(("B", 1, 2))

@@ -19,9 +19,22 @@ ACT = mybir.ActivationFunctionType
 
 P = 128
 PACK = 4
-W = 512
-NG = D // W
-SG = S // W
+RUN = 8
+W = P * PACK
+NODE_GROUPS = D // W
+SEED_GROUPS = S // W
+QUADRANT = 32
+
+SCORE_TILES = {"y00": (0, 0, 512), "y01": (1, 0, 512), "y02": (2, 0, 512), "y10": (0, 512, 512), "y11": (1, 512, 512), "y12": (2, 512, 512)}
+
+ORDER = """
+ls02 identB identF loadQ1 loadW loadQs loadP0 loadPs loadQ0 ls12 is02@V turnW orderQ1 ls01 is12@H
+qs02 loadP1 orderQ0 loadT mh01 mh00 ls11 mh01+ mh00+ mh10 ls10 is10@V ih00@V is11@S scaleT is01@G
+qs01 ls00 ih01@S qh00 qs10 qs11 qh01 qs12 mh11 mh11+ is00@H my01 qs00 ih11@H my01+ mh10+ my00 qh11
+my02 my02+ ih10@H qh10 ty01+@SS ty01@SV iy01@H my00+ ty02+@SS ty02@VV qy01 my11 my11+ iy00@H
+ty00+@SS iy02@G ty00@SV my10 ty11+@SV my10+ ty11@SS qy00 qy02 my12 storeS0 ty10+@SV my12+ ty10@SS
+iy11@G ty12@SV iy10@H ty12+@VV qy11 iy12@S qy10 qy12 storeS1
+"""
 
 
 def tile_cubed_walk_seed_scores_h2_kernel(
@@ -37,328 +50,246 @@ def tile_cubed_walk_seed_scores_h2_kernel(
         def kept(name, shape, dtype):
             return keep.tile(shape, dtype, name=name, align_bytes=64)
 
-        q_raw = [kept("q_raw%d" % g, [P, NG, 2 * W], U8) for g in range(NG)]
-        qs_raw = kept("qs_raw", [P, NG, D], U8)
-        ps = kept("ps", [P, NG, D], U8)
-        p_words = [kept("p_words%d" % h, [P, NG, W], U32) for h in range(NG)]
-        q_words = [kept("q_words%d" % g, [P, NG, 2 * W], U8) for g in range(NG)]
-        qs = [kept("qs%d" % g, [P, NG, W], U8) for g in range(NG)]
-        w_rows = kept("w_rows", [P, NG, P], BF16)
-        ident_h = kept("ident_h", [P, P], BF16)
-        w_col = kept("w_col", [P, NG, PACK], F32)
-        t_raw = kept("t_raw", [P, SG, PACK], BF16)
-        t_col = kept("t_col", [P, SG, PACK], F32)
-        t_bias = kept("t_bias", [P, SG, PACK], F32)
-        ident = kept("ident", [P, P], F32)
+        halves = range(NODE_GROUPS)
+        p_words = [kept("p_words%d" % h, [P, NODE_GROUPS, W], U32) for h in halves]
+        p_scales = kept("p_scales", [P, NODE_GROUPS, D], U8)
+        q_raw = [kept("q_raw%d" % g, [P, NODE_GROUPS, 2 * W], U8) for g in halves]
+        q_scales_raw = kept("q_scales_raw", [P, NODE_GROUPS, D], U8)
+        q_words = [kept("q_words%d" % g, [P, NODE_GROUPS, 2 * W], U8) for g in halves]
+        q_scales = [kept("q_scales%d" % g, [P, NODE_GROUPS, W], U8) for g in halves]
+        weight_rows = kept("weight_rows", [P, NODE_GROUPS, P], BF16)
+        weight = kept("weight", [P, NODE_GROUPS, PACK], F32)
+        thr = kept("thr", [P, SEED_GROUPS, PACK], BF16)
+        thr_bias = kept("thr_bias", [P, SEED_GROUPS, PACK], F32)
+        ident_bf16 = kept("ident_bf16", [P, P], BF16)
+        ident_f32 = kept("ident_f32", [P, P], F32)
         warm = kept("warm", [P, 1], F32)
-        s_first = [kept("s_first%d" % g, [P, PACK, W], BF16) for g in range(NG)]
-        s_rest = [kept("s_rest%d" % g, [P, PACK, S - W], BF16) for g in range(NG)]
-        s_codes = {}
-        s_scales = {}
-        s_grouped = {}
-        for sg in range(SG):
-            for g in range(NG):
-                s_codes[g, sg] = kept("s_codes%d%d" % (g, sg), [P, W], U32)
-                s_scales[g, sg] = kept("s_scales%d%d" % (g, sg), [P, W], U8)
-        h_codes = {}
-        h_scales = {}
-        for h in range(NG):
-            for g in range(NG):
-                h_codes[h, g] = kept("h_codes%d%d" % (h, g), [P, W], U32)
-                h_scales[h, g] = kept("h_scales%d%d" % (h, g), [P, W], U8)
-        y_codes = {}
-        for h in range(NG):
-            for sg in range(SG):
-                y_codes[h, sg] = kept("y_codes%d%d" % (h, sg), [P, W], U32)
-        y_scales = [kept("y_scales%d" % h, [P, SG, W], U8) for h in range(NG)]
+        y_scales = [kept("y_scales%d" % h, [P, SEED_GROUPS, W], U8) for h in halves]
+
+        slots = {}
+        packed = {}
+        codes = {}
+        scales = {}
+        for g in halves:
+            for s in range(SEED_GROUPS):
+                name = "s%d%d" % (g, s)
+                slots[name] = kept("raw_" + name, [P, PACK, W], BF16)
+                codes[name] = kept("codes_" + name, [P, W], U32)[:]
+                scales[name] = kept("scales_" + name, [P, W], U8)[:]
+            for h in halves:
+                name = "h%d%d" % (h, g)
+                codes[name] = kept("codes_" + name, [P, W], U32)[:]
+                scales[name] = kept("scales_" + name, [P, W], U8)[:]
+        for name, (s, m0, width) in SCORE_TILES.items():
+            codes[name] = kept("codes_" + name, [P, width], U32)[:]
+            scales[name] = y_scales[m0 // W][:, s, m0 % W : m0 % W + width]
 
         nc.vector.memset(warm[:], 0.0)
-        nc.gpsimd.memset(ps[:].rearrange("p g n -> p (g n)").bitcast(I32), 0)
-        nc.vector.memset(qs_raw[:].rearrange("p g n -> p (g n)").bitcast(I32), 0)
-        nc.vector.memset(w_rows[:], 0.0)
         nc.scalar.activation(out=warm[:], in_=warm[:], func=ACT.Square)
+        nc.vector.memset(q_scales_raw[:].rearrange("p c n -> p (c n)").bitcast(I32), 0)
+        nc.vector.memset(p_scales[:].rearrange("p c n -> p (c n)").bitcast(I32), 0)
+        nc.vector.memset(weight_rows[:], 0.0)
 
-        def load_p(h, queue):
-            src = left_words.rearrange("g p n t -> p g (n t)")[:, :, h * W * PACK : (h + 1) * W * PACK]
-            queue.dma_start(out=p_words[h][:].bitcast(I32), in_=src.bitcast(I32))
+        def load_p(h):
+            src = left_words.rearrange("c p n t -> p c (n t)")[:, :, h * W * PACK : (h + 1) * W * PACK]
+            nc.sync.dma_start(out=p_words[h][:].bitcast(I32), in_=src.bitcast(I32))
 
-        def load_scales(plane, src, q, queue):
-            rows = src.rearrange("g r n -> r g n")[4 * q : 4 * q + 4]
-            queue.dma_start(out=plane[32 * q : 32 * q + 4].bitcast(I32), in_=rows.bitcast(I32))
-
-        def load_seeds(g, c0, c1, t, queue):
-            src = seeds[g * W : (g + 1) * W, c0:c1].rearrange("(b t r) s -> t b r s", t=PACK, r=8)
-            queue.dma_start(out=(s_first if c0 == 0 else s_rest)[g][:, t, :], in_=src[t])
-
-        def load_q(g, queue):
+        def load_q(g):
             src = right_words.rearrange("c p n -> p c n")[:, :, g * 2 * W : (g + 1) * 2 * W]
-            queue.dma_start(out=q_raw[g][:].bitcast(I32), in_=src.bitcast(I32))
+            nc.sync.dma_start(out=q_raw[g][:].bitcast(I32), in_=src.bitcast(I32))
 
+        def load_scales(plane, src):
+            rows = src.rearrange("c r n -> r c n")
+            for q in range(P // QUADRANT):
+                live = plane[QUADRANT * q : QUADRANT * q + 4]
+                nc.sync.dma_start(out=live.bitcast(I32), in_=rows[4 * q : 4 * q + 4].bitcast(I32))
 
-        def load_w(queue):
-            src = node_weight.rearrange("(b t r) -> t b r", t=PACK, r=8)
-            queue.dma_start(out=w_rows[:PACK].rearrange("t g (b r) -> t (g b) r", r=8), in_=src)
+        def load_seeds(g, s):
+            rows = seeds[g * W : (g + 1) * W, s * W : (s + 1) * W].rearrange("(b t r) n -> t b r n", t=PACK, r=RUN)
+            for t in range(PACK):
+                nc.sync.dma_start(out=slots["s%d%d" % (g, s)][:, t, :], in_=rows[t])
 
-        def load_t(queue):
-            queue.dma_start(out=t_raw[:], in_=threshold.rearrange("(g p t) -> p g t", p=P, t=PACK))
+        def load_weight():
+            src = node_weight.rearrange("(b t r) -> t b r", t=PACK, r=RUN)
+            nc.sync.dma_start(out=weight_rows[:PACK].rearrange("t g (b r) -> t (g b) r", r=RUN), in_=src)
 
-        def permute_q(g):
-            nc.vector.tensor_copy(
-                out=q_words[g][:].bitcast(I32).rearrange("p c (t b r) -> p c t b r", t=PACK, r=4),
-                in_=q_raw[g][:].bitcast(I32).rearrange("p c (b t r) -> p c t b r", t=PACK, r=4),
-            )
-            nc.vector.tensor_copy(
-                out=qs[g][:].bitcast(I32).rearrange("p c (t b r) -> p c t b r", t=PACK, r=2),
-                in_=qs_raw[:, :, g * W : (g + 1) * W].bitcast(I32).rearrange("p c (b t r) -> p c t b r", t=PACK, r=2),
-            )
+        def load_threshold():
+            nc.sync.dma_start(out=thr[:], in_=threshold.rearrange("(s p t) -> p s t", p=P, t=PACK))
 
-        def weights():
-            bank = psum.tile([P, NG, P], BF16, name="bank")
-            for g in range(NG):
-                nc.tensor.transpose(bank[:, g, :], w_rows[:, g, :], ident_h[:])
-            nc.vector.tensor_copy(out=w_col[:], in_=bank[:, :, :PACK])
-
-        def interleave(dst, src, engine):
-            if engine == "S":
-                nc.scalar.copy(out=dst, in_=src)
-            elif engine == "V":
-                nc.vector.tensor_copy(out=dst, in_=src)
-            else:
-                nc.gpsimd.tensor_scalar(out=dst, in0=src, scalar1=1.0, scalar2=1.0, op0=ALU.mult, op1=ALU.mult)
-
-        def grouped_tile(engine):
-            return work.tile([P, W, PACK], BF16, name="grouped" + engine, bufs=1 if engine == "G" else 2, align_bytes=64)
-
-        def seeds_group(g, sg, engine):
-            grouped = grouped_tile(engine)
-            s_grouped[g, sg] = grouped
-            dst = grouped[:].rearrange("p (t m) j -> p t m j", t=PACK)
-            src = (s_first[g][:] if sg == 0 else s_rest[g][:, :, (sg - 1) * W : sg * W]).rearrange("p j (m t) -> p t m j", t=PACK)
-            interleave(dst, src, engine)
-
-        def quantize(codes, scales, grouped):
-            nc.vector.quantize_mx(out=codes.bitcast(FP8X4), scales=scales, in_=grouped[:].rearrange("p m t -> p (m t)"))
-
-        def seeds_quant(g, sg):
-            quantize(s_codes[g, sg][:], s_scales[g, sg][:], s_grouped[g, sg])
-
-        rows = {}
-        grouped_of = {}
-
-        def walk(h, g, t):
-            if t == 0:
-                rows["A", h, g] = work.tile([P, PACK, W], BF16, name="hb", bufs=3, align_bytes=64)
-            hb = rows["A", h, g]
-            if True:
-                bank = psum.tile([P, W], F32, name="bank")
-                for c in range(NG):
-                    nc.tensor.matmul_mx(
-                        out=bank[:],
-                        lhsT=q_words[g][:, c, t * 2 * P : (t + 1) * 2 * P].bitcast(FP4X4),
-                        lhsT_scale=qs[g][:, c, t * P : (t + 1) * P],
-                        rhs=p_words[h][:, c, :].bitcast(FP8X4),
-                        rhs_scale=ps[:, c, h * W : (h + 1) * W],
-                        start=(c == 0),
-                        stop=(c == NG - 1),
-                    )
-                sq = work.tile([P, W], F32, name="sq", bufs=4)
-                nc.scalar.activation(out=sq[:], in_=bank[:], func=ACT.Square)
-                nc.vector.scalar_tensor_tensor(
-                    out=hb[:, t, :], in0=bank[:], scalar=w_col[:, g, t : t + 1], in1=sq[:], op0=ALU.mult, op1=ALU.mult
+        def reorder_q(g):
+            for dst, src, run in (
+                (q_words[g][:], q_raw[g][:], RUN // 2),
+                (q_scales[g][:], q_scales_raw[:, :, g * W : (g + 1) * W], RUN // 4),
+            ):
+                nc.vector.tensor_copy(
+                    out=dst.bitcast(I32).rearrange("p c (t b r) -> p c t b r", t=PACK, r=run),
+                    in_=src.bitcast(I32).rearrange("p c (b t r) -> p c t b r", t=PACK, r=run),
                 )
 
-        def score(h, sg, t):
-            if t == 0:
-                rows["B", h, sg] = work.tile([P, PACK, W], F32, name="yt", bufs=3)
-            yt = rows["B", h, sg]
-            if True:
-                bank = psum.tile([P, W], F32, name="bank")
-                for c in range(NG):
-                    nc.tensor.matmul_mx(
-                        out=bank[:],
-                        lhsT=s_codes[c, sg][:, t * P : (t + 1) * P].bitcast(FP8X4),
-                        lhsT_scale=s_scales[c, sg][:, t * P : (t + 1) * P],
-                        rhs=h_codes[h, c][:].bitcast(FP8X4),
-                        rhs_scale=h_scales[h, c][:],
-                        start=(c == 0),
-                        stop=(c == NG - 1),
-                    )
-                low = work.tile([P, W], F32, name="sq", bufs=4)
+        def turn_weight():
+            bank = psum.tile([P, NODE_GROUPS, P], BF16, name="bank")
+            for g in halves:
+                nc.tensor.transpose(bank[:, g, :], weight_rows[:, g, :], ident_bf16[:])
+            nc.scalar.copy(out=weight[:], in_=bank[:, :, :PACK])
+
+        def scale_threshold():
+            nc.scalar.activation(out=thr_bias[:], in_=thr[:], func=ACT.Copy, scale=-SLOPE)
+
+        def product(width, operands):
+            bank = psum.tile([P, width], F32, name="bank")
+            for c in halves:
+                lhsT, lhsT_scale, rhs, rhs_scale = operands(c)
+                nc.tensor.matmul_mx(
+                    out=bank[:],
+                    lhsT=lhsT,
+                    lhsT_scale=lhsT_scale,
+                    rhs=rhs,
+                    rhs_scale=rhs_scale,
+                    start=(c == 0),
+                    stop=(c == NODE_GROUPS - 1),
+                )
+            return bank
+
+        def cube(h, g, first):
+            name = "h%d%d" % (h, g)
+            if first == 0:
+                slots[name] = work.tile([P, PACK, W], BF16, name="h_slots", bufs=3)
+            for t in (first, first + 1):
+                bank = product(
+                    W,
+                    lambda c: (
+                        q_words[g][:, c, t * 2 * P : (t + 1) * 2 * P].bitcast(FP4X4),
+                        q_scales[g][:, c, t * P : (t + 1) * P],
+                        p_words[h][:, c, :].bitcast(FP8X4),
+                        p_scales[:, c, h * W : (h + 1) * W],
+                    ),
+                )
+                square = work.tile([P, W], F32, name="partner", bufs=4)
+                nc.scalar.activation(out=square[:], in_=bank[:], func=ACT.Square)
+                nc.vector.scalar_tensor_tensor(
+                    out=slots[name][:, t, :],
+                    in0=bank[:],
+                    scalar=weight[:, g, t : t + 1],
+                    in1=square[:],
+                    op0=ALU.mult,
+                    op1=ALU.mult,
+                )
+
+        def score(name, first):
+            s, m0, width = SCORE_TILES[name]
+            h, cols = m0 // W, slice(m0 % W, m0 % W + width)
+            if first == 0:
+                slots[name] = work.tile([P, PACK, width], F32, name="y_slots", bufs=3)
+            for t in (first, first + 1):
+                bank = product(
+                    width,
+                    lambda g: (
+                        codes["s%d%d" % (g, s)][:, t * P : (t + 1) * P].bitcast(FP8X4),
+                        scales["s%d%d" % (g, s)][:, t * P : (t + 1) * P],
+                        codes["h%d%d" % (h, g)][:, cols].bitcast(FP8X4),
+                        scales["h%d%d" % (h, g)][:, cols],
+                    ),
+                )
+                sloped = work.tile([P, width], F32, name="partner", bufs=4)
                 nc.scalar.activation(
-                    out=low[:], in_=bank[:], func=ACT.Identity, scale=SLOPE, bias=t_bias[:, sg, t : t + 1]
+                    out=sloped[:], in_=bank[:], func=ACT.Identity, scale=SLOPE, bias=thr_bias[:, s, t : t + 1]
                 )
                 nc.vector.scalar_tensor_tensor(
-                    out=yt[:, t, :], in0=bank[:], scalar=t_col[:, sg, t : t + 1], in1=low[:], op0=ALU.subtract, op1=ALU.max
+                    out=slots[name][:, t, :],
+                    in0=bank[:],
+                    scalar=thr[:, s, t : t + 1],
+                    in1=sloped[:],
+                    op0=ALU.subtract,
+                    op1=ALU.max,
                 )
 
-        def group(key, engine):
-            grouped = grouped_tile(engine)
-            grouped_of[key] = grouped
-            interleave(
-                grouped[:].rearrange("p (c i) t -> p c t i", i=4),
-                rows[key][:].rearrange("p t (c i) -> p c t i", i=4),
-                engine,
-            )
-
-        def quant(key):
-            kind, h, g = key
-            if kind == "A":
-                quantize(h_codes[h, g][:], h_scales[h, g][:], grouped_of[key])
+        def interleave(name, engine):
+            on_gpsimd = engine in "GH"
+            width = slots[name].shape[2]
+            tile = work.tile([P, width, PACK], BF16, name="packed" + engine, bufs=1 if on_gpsimd else 2, align_bytes=64)
+            packed[name] = tile
+            if name[0] == "s":
+                walk = "p m t i"
+                dst = tile[:].rearrange("p (i m) t -> " + walk, i=PACK)
+                src = slots[name][:].rearrange("p t (m i) -> " + walk, i=PACK)
             else:
-                quantize(y_codes[h, g][:], y_scales[h][:, g, :], grouped_of[key])
-                dst = out_1[g].rearrange("p m t -> p (m t)")[:, h * W * PACK : (h + 1) * W * PACK]
-                nc.sync.dma_start(out=dst.bitcast(I32), in_=y_codes[h, g][:].bitcast(I32))
-                if g == SG - 1:
-                    for q in range(4):
-                        dst = out_2.rearrange("g r m -> r g m")[4 * q : 4 * q + 4, :, h * W : (h + 1) * W]
-                        nc.sync.dma_start(out=dst.bitcast(I32), in_=y_scales[h][32 * q : 32 * q + 4].bitcast(I32))
+                walk = "p m t i"
+                dst = tile[:].rearrange("p (m i) t -> " + walk, i=PACK)
+                src = slots[name][:].rearrange("p t (m i) -> " + walk, i=PACK)
+            if on_gpsimd:
+                nc.gpsimd.tensor_scalar(out=dst, in0=src, scalar1=1.0, scalar2=1.0, op0=ALU.mult, op1=ALU.mult)
+            elif engine == "S":
+                nc.scalar.copy(out=dst, in_=src)
+            else:
+                nc.vector.tensor_copy(out=dst, in_=src)
 
-        def turn(h, sg, mt, engine):
-            yt = rows["B", h, sg]
-            if True:
+        def quantize(name):
+            nc.vector.quantize_mx(
+                out=codes[name].bitcast(FP8X4), scales=scales[name], in_=packed[name][:].rearrange("p m t -> p (m t)")
+            )
+            if name in SCORE_TILES:
+                s, m0, width = SCORE_TILES[name]
+                dst = out_1[s].rearrange("p m t -> p (m t)")[:, m0 * PACK : (m0 + width) * PACK]
+                nc.sync.dma_start(out=dst.bitcast(I32), in_=codes[name].bitcast(I32))
+
+        def store_scales(h):
+            rows = out_2.rearrange("s r m -> r s m")[:, :, h * W : (h + 1) * W]
+            for q in range(P // QUADRANT):
+                live = y_scales[h][QUADRANT * q : QUADRANT * q + 4]
+                nc.sync.dma_start(out=rows[4 * q : 4 * q + 4].bitcast(I32), in_=live.bitcast(I32))
+
+        def turn(name, first, engines):
+            s, m0, width = SCORE_TILES[name]
+            for j, engine in zip((first, first + 1), engines):
                 bank = psum.tile([P, PACK, P], F32, name="bank")
                 for t in range(PACK):
-                    nc.tensor.transpose(bank[:, t, :], yt[:, t, mt * P : (mt + 1) * P], ident[:])
-                y = work.tile([P, W], F32, name="y", bufs=8)
+                    nc.tensor.transpose(bank[:, t, :], slots[name][:, t, j * P : (j + 1) * P], ident_f32[:])
+                y = work.tile([P, W], F32, name="y_rows", bufs=8)
                 dst = y[:].rearrange("m (p t) -> m p t", t=PACK)
                 src = bank[:].rearrange("m t p -> m p t")
-                if engine == "V":
-                    nc.vector.tensor_copy(out=dst, in_=src)
-                else:
+                if engine == "S":
                     nc.scalar.copy(out=dst, in_=src)
-                m0 = h * W + mt * P
-                nc.sync.dma_start(out=out_0[m0 : m0 + P, sg * W : (sg + 1) * W], in_=y[:])
+                else:
+                    nc.vector.tensor_copy(out=dst, in_=src)
+                row = m0 + j * P
+                nc.sync.dma_start(out=out_0[row : row + P, s * W : (s + 1) * W], in_=y[:])
 
-        load_seeds(0, W, S, 0, nc.sync)
-        load_seeds(0, W, S, 1, nc.sync)
-        load_seeds(0, W, S, 2, nc.sync)
-        load_seeds(0, W, S, 3, nc.sync)
-        load_q(0, nc.sync)
-        load_scales(qs_raw, right_scales, 0, nc.sync)
-        load_scales(qs_raw, right_scales, 1, nc.sync)
-        load_scales(qs_raw, right_scales, 2, nc.sync)
-        load_scales(qs_raw, right_scales, 3, nc.sync)
-        seeds_group(0, 2, "V")
-        load_seeds(1, W, S, 0, nc.sync)
-        load_seeds(1, W, S, 1, nc.sync)
-        load_seeds(1, W, S, 2, nc.sync)
-        load_seeds(1, W, S, 3, nc.sync)
-        seeds_group(0, 1, "S")
-        load_t(nc.sync)
-        load_w(nc.sync)
-        permute_q(0)
-        load_p(0, nc.sync)
-        make_identity(nc, ident_h[:])
-        load_scales(ps, left_scales, 0, nc.sync)
-        load_scales(ps, left_scales, 1, nc.sync)
-        load_scales(ps, left_scales, 2, nc.sync)
-        load_scales(ps, left_scales, 3, nc.sync)
-        seeds_quant(0, 2)
-        load_q(1, nc.sync)
-        seeds_quant(0, 1)
-        seeds_group(1, 1, "S")
-        load_seeds(1, 0, W, 0, nc.sync)
-        load_seeds(1, 0, W, 1, nc.sync)
-        load_seeds(1, 0, W, 2, nc.sync)
-        load_seeds(1, 0, W, 3, nc.sync)
-        load_seeds(0, 0, W, 0, nc.sync)
-        load_seeds(0, 0, W, 1, nc.sync)
-        load_seeds(0, 0, W, 2, nc.sync)
-        load_seeds(0, 0, W, 3, nc.sync)
-        seeds_group(1, 2, "V")
-        nc.vector.tensor_copy(out=t_col[:], in_=t_raw[:])
-        nc.vector.tensor_scalar_mul(out=t_bias[:], in0=t_raw[:], scalar1=-SLOPE)
-        weights()
-        seeds_quant(1, 2)
-        permute_q(1)
-        seeds_quant(1, 1)
-        walk(0, 0, 0)
-        walk(0, 0, 1)
-        walk(0, 0, 2)
-        walk(0, 0, 3)
-        seeds_group(0, 0, "V")
-        walk(0, 1, 0)
-        walk(0, 1, 1)
-        seeds_group(1, 0, "V")
-        group(("A", 0, 0), "S")
-        walk(0, 1, 2)
-        walk(0, 1, 3)
-        load_p(1, nc.sync)
-        seeds_quant(1, 0)
-        walk(1, 1, 0)
-        walk(1, 1, 1)
-        walk(1, 0, 0)
-        walk(1, 0, 1)
-        quant(("A", 0, 0))
-        group(("A", 0, 1), "S")
-        seeds_quant(0, 0)
-        make_identity(nc, ident[:])
-        quant(("A", 0, 1))
-        walk(1, 1, 2)
-        walk(1, 1, 3)
-        walk(1, 0, 2)
-        walk(1, 0, 3)
-        score(0, 2, 0)
-        score(0, 2, 1)
-        score(0, 0, 0)
-        score(0, 0, 1)
-        score(0, 2, 2)
-        score(0, 2, 3)
-        group(("A", 1, 0), "V")
-        score(0, 0, 2)
-        score(0, 0, 3)
-        score(0, 1, 0)
-        score(0, 1, 1)
-        turn(0, 2, 2, "S")
-        turn(0, 2, 3, "S")
-        score(0, 1, 2)
-        score(0, 1, 3)
-        quant(("A", 1, 0))
-        group(("A", 1, 1), "V")
-        group(("B", 0, 0), "V")
-        turn(0, 0, 2, "S")
-        turn(0, 0, 3, "S")
-        turn(0, 2, 0, "S")
-        turn(0, 2, 1, "S")
-        quant(("A", 1, 1))
-        turn(0, 0, 0, "S")
-        turn(0, 0, 1, "S")
-        quant(("B", 0, 0))
-        group(("B", 0, 2), "S")
-        turn(0, 1, 2, "V")
-        turn(0, 1, 3, "S")
-        turn(0, 1, 0, "V")
-        turn(0, 1, 1, "S")
-        group(("B", 0, 1), "V")
-        score(1, 0, 0)
-        score(1, 0, 1)
-        quant(("B", 0, 1))
-        score(1, 0, 2)
-        score(1, 0, 3)
-        score(1, 1, 0)
-        score(1, 1, 1)
-        score(1, 1, 2)
-        score(1, 1, 3)
-        turn(1, 0, 2, "S")
-        turn(1, 0, 3, "S")
-        turn(1, 0, 0, "V")
-        turn(1, 0, 1, "S")
-        quant(("B", 0, 2))
-        score(1, 2, 0)
-        score(1, 2, 1)
-        turn(1, 1, 2, "S")
-        turn(1, 1, 3, "V")
-        score(1, 2, 2)
-        score(1, 2, 3)
-        group(("B", 1, 1), "V")
-        turn(1, 1, 0, "S")
-        turn(1, 1, 1, "S")
-        group(("B", 1, 0), "V")
-        turn(1, 2, 2, "S")
-        turn(1, 2, 3, "S")
-        turn(1, 2, 0, "S")
-        turn(1, 2, 1, "V")
-        quant(("B", 1, 1))
-        quant(("B", 1, 0))
-        group(("B", 1, 2), "S")
-        quant(("B", 1, 2))
+        def run(step):
+            word, engines = (step + "@").split("@")[:2]
+            verb, name = word[0], word[1:].replace("+", "")
+            first = 2 if "+" in word else 0
+            if step in single:
+                single[step]()
+            elif verb == "l":
+                load_seeds(int(name[1]), int(name[2]))
+            elif verb == "m" and name[0] == "h":
+                cube(int(name[1]), int(name[2]), first)
+            elif verb == "m":
+                score(name, first)
+            elif verb == "i":
+                interleave(name, engines)
+            elif verb == "q":
+                quantize(name)
+            else:
+                turn(name, first, engines)
+
+        single = {
+            "identB": lambda: make_identity(nc, ident_bf16[:]),
+            "identF": lambda: make_identity(nc, ident_f32[:]),
+            "loadP0": lambda: load_p(0),
+            "loadP1": lambda: load_p(1),
+            "loadQ0": lambda: load_q(0),
+            "loadQ1": lambda: load_q(1),
+            "loadPs": lambda: load_scales(p_scales, left_scales),
+            "loadQs": lambda: load_scales(q_scales_raw, right_scales),
+            "loadW": load_weight,
+            "loadT": load_threshold,
+            "orderQ0": lambda: reorder_q(0),
+            "orderQ1": lambda: reorder_q(1),
+            "turnW": turn_weight,
+            "scaleT": scale_threshold,
+            "storeS0": lambda: store_scales(0),
+            "storeS1": lambda: store_scales(1),
+        }
+        for step in ORDER.split():
+            run(step)

@@ -25,15 +25,17 @@ NODE_GROUPS = D // W
 SEED_GROUPS = S // W
 QUADRANT = 32
 
-SCORE_TILES = {"y00": (0, 0, 512), "y01": (1, 0, 512), "y02": (2, 0, 512), "y10": (0, 512, 512), "y11": (1, 512, 512), "y12": (2, 512, 512)}
+SCORE_TILES = {"y00": (0, 0, 512), "y01": (1, 0, 512), "y02": (2, 0, 512), "y10": (0, 512, 512), "y12": (2, 512, 512), "y11a": (1, 512, 256), "y11b": (1, 768, 256)}
+
+RING = {"bank": 8, "h_slots": 4, "y_slots": 5, "partner": 6, "y_rows": 8, "packedV": 3, "packedS": 2, "packedG": 1, "packedH": 1}
 
 ORDER = """
-ls02 identB identF loadQ1 loadW loadQs loadP0 loadPs loadQ0 ls12 is02@V turnW orderQ1 ls01 is12@H
-qs02 loadP1 orderQ0 loadT mh01 mh00 ls11 mh01+ mh00+ mh10 ls10 is10@V ih00@V is11@S scaleT is01@G
-qs01 ls00 ih01@S qh00 qs10 qs11 qh01 qs12 mh11 mh11+ is00@H my01 qs00 ih11@H my01+ mh10+ my00 qh11
-my02 my02+ ih10@H qh10 ty01+@SS ty01@SV iy01@H my00+ ty02+@SS ty02@VV qy01 my11 my11+ iy00@H
-ty00+@SS iy02@G ty00@SV my10 ty11+@SV my10+ ty11@SS qy00 qy02 my12 storeS0 ty10+@SV my12+ ty10@SS
-iy11@G ty12@SV iy10@H ty12+@VV qy11 iy12@S qy10 qy12 storeS1
+ls10 loadQ0 is10@S loadW loadQs loadP0 orderQ0 loadPs loadQ1 turnW ls00 loadP1 qs10 ls11 ls01
+orderQ1 mh00 mh00+ mh01 mh01+ mh10 mh11 is01@V loadT ih00@V ih01@S is00@H qs01 scaleT ls12 qh00 qh01
+qs00 is11@G ls02 is02@S is12@H qs11 mh11+ mh10+ my01 qs12 ih11@H qs02 my01+ my00 my00+ my02 ih10@G
+ty01@SS my02+ ty01+@SS qh11 ty00+@SS qh10 ty00@SV ty02@VS ty02+@VV iy01@H iy00@G my10 my10+ my12
+ty10@SS qy01 qy00 my12+ ty10+@SV my11a ty12@SV ty12+@SV iy02@H my11a+ my11b my11b+ ty11a@SV iy10@S
+iy12@G qy02 qy12 iy11a@H storeS0 ty11b@VV qy10 iy11b@S qy11a qy11b storeS1
 """
 
 
@@ -43,12 +45,18 @@ def tile_cubed_walk_seed_scores_h2_kernel(
     nc = tc.nc
     with ExitStack() as ctx:
         keep = ctx.enter_context(tc.tile_pool(name="keep", bufs=1))
-        work = ctx.enter_context(tc.tile_pool(name="work", bufs=2))
-        psum = ctx.enter_context(tc.psum_pool(name="psum", bufs=8))
+        work = ctx.enter_context(tc.tile_pool(name="work", bufs=1))
+        psum = ctx.enter_context(tc.psum_pool(name="psum", bufs=1))
         ctx.enter_context(tc.manual_schedule())
 
         def kept(name, shape, dtype):
             return keep.tile(shape, dtype, name=name, align_bytes=64)
+
+        turns = {}
+
+        def ring(pool, name, shape, dtype):
+            turns[name] = (turns.get(name, -1) + 1) % RING[name]
+            return pool.tile(shape, dtype, name="%s%d" % (name, turns[name]), align_bytes=64 if pool is work else None)
 
         halves = range(NODE_GROUPS)
         p_words = [kept("p_words%d" % h, [P, NODE_GROUPS, W], U32) for h in halves]
@@ -89,6 +97,9 @@ def tile_cubed_walk_seed_scores_h2_kernel(
         nc.vector.memset(q_scales_raw[:].rearrange("p c n -> p (c n)").bitcast(I32), 0)
         nc.vector.memset(p_scales[:].rearrange("p c n -> p (c n)").bitcast(I32), 0)
         nc.vector.memset(weight_rows[:], 0.0)
+        for ident in (ident_bf16, ident_f32):
+            nc.vector.memset(ident[:], 0.0)
+            make_identity(nc, ident[:], nomemset=True)
 
         def load_p(h):
             src = left_words.rearrange("c p n t -> p c (n t)")[:, :, h * W * PACK : (h + 1) * W * PACK]
@@ -127,7 +138,7 @@ def tile_cubed_walk_seed_scores_h2_kernel(
                 )
 
         def turn_weight():
-            bank = psum.tile([P, NODE_GROUPS, P], BF16, name="bank")
+            bank = ring(psum, "bank", [P, NODE_GROUPS, P], BF16)
             for g in halves:
                 nc.tensor.transpose(bank[:, g, :], weight_rows[:, g, :], ident_bf16[:])
             nc.scalar.copy(out=weight[:], in_=bank[:, :, :PACK])
@@ -136,7 +147,7 @@ def tile_cubed_walk_seed_scores_h2_kernel(
             nc.scalar.activation(out=thr_bias[:], in_=thr[:], func=ACT.Copy, scale=-SLOPE)
 
         def product(width, operands):
-            bank = psum.tile([P, width], F32, name="bank")
+            bank = ring(psum, "bank", [P, width], F32)
             for c in halves:
                 lhsT, lhsT_scale, rhs, rhs_scale = operands(c)
                 nc.tensor.matmul_mx(
@@ -153,7 +164,7 @@ def tile_cubed_walk_seed_scores_h2_kernel(
         def cube(h, g, first):
             name = "h%d%d" % (h, g)
             if first == 0:
-                slots[name] = work.tile([P, PACK, W], BF16, name="h_slots", bufs=3)
+                slots[name] = ring(work, "h_slots", [P, PACK, W], BF16)
             for t in (first, first + 1):
                 bank = product(
                     W,
@@ -164,7 +175,7 @@ def tile_cubed_walk_seed_scores_h2_kernel(
                         p_scales[:, c, h * W : (h + 1) * W],
                     ),
                 )
-                square = work.tile([P, W], F32, name="partner", bufs=4)
+                square = ring(work, "partner", [P, W], F32)
                 nc.scalar.activation(out=square[:], in_=bank[:], func=ACT.Square)
                 nc.vector.scalar_tensor_tensor(
                     out=slots[name][:, t, :],
@@ -179,7 +190,7 @@ def tile_cubed_walk_seed_scores_h2_kernel(
             s, m0, width = SCORE_TILES[name]
             h, cols = m0 // W, slice(m0 % W, m0 % W + width)
             if first == 0:
-                slots[name] = work.tile([P, PACK, width], F32, name="y_slots", bufs=3)
+                slots[name] = ring(work, "y_slots", [P, PACK, width], F32)
             for t in (first, first + 1):
                 bank = product(
                     width,
@@ -190,7 +201,7 @@ def tile_cubed_walk_seed_scores_h2_kernel(
                         scales["h%d%d" % (h, g)][:, cols],
                     ),
                 )
-                sloped = work.tile([P, width], F32, name="partner", bufs=4)
+                sloped = ring(work, "partner", [P, width], F32)
                 nc.scalar.activation(
                     out=sloped[:], in_=bank[:], func=ACT.Identity, scale=SLOPE, bias=thr_bias[:, s, t : t + 1]
                 )
@@ -206,7 +217,7 @@ def tile_cubed_walk_seed_scores_h2_kernel(
         def interleave(name, engine):
             on_gpsimd = engine in "GH"
             width = slots[name].shape[2]
-            tile = work.tile([P, width, PACK], BF16, name="packed" + engine, bufs=1 if on_gpsimd else 2, align_bytes=64)
+            tile = ring(work, "packed" + engine, [P, width, PACK], BF16)
             packed[name] = tile
             if name[0] == "s":
                 walk = "p m t i"
@@ -241,10 +252,10 @@ def tile_cubed_walk_seed_scores_h2_kernel(
         def turn(name, first, engines):
             s, m0, width = SCORE_TILES[name]
             for j, engine in zip((first, first + 1), engines):
-                bank = psum.tile([P, PACK, P], F32, name="bank")
+                bank = ring(psum, "bank", [P, PACK, P], F32)
                 for t in range(PACK):
                     nc.tensor.transpose(bank[:, t, :], slots[name][:, t, j * P : (j + 1) * P], ident_f32[:])
-                y = work.tile([P, W], F32, name="y_rows", bufs=8)
+                y = ring(work, "y_rows", [P, W], F32)
                 dst = y[:].rearrange("m (p t) -> m p t", t=PACK)
                 src = bank[:].rearrange("m t p -> m p t")
                 if engine == "S":
@@ -274,8 +285,6 @@ def tile_cubed_walk_seed_scores_h2_kernel(
                 turn(name, first, engines)
 
         single = {
-            "identB": lambda: make_identity(nc, ident_bf16[:]),
-            "identF": lambda: make_identity(nc, ident_f32[:]),
             "loadP0": lambda: load_p(0),
             "loadP1": lambda: load_p(1),
             "loadQ0": lambda: load_q(0),

@@ -21,13 +21,33 @@ P = 128
 PACK = 4
 RUN = 8
 W = P * PACK
+FP4_BYTES = 2
+QUADRANT = 32
+SCALE_ROWS = QUADRANT // RUN
 NODE_GROUPS = D // W
 SEED_GROUPS = S // W
-QUADRANT = 32
 
-SCORE_TILES = {"y00": (0, 0, 512), "y01": (1, 0, 512), "y02": (2, 0, 512), "y10": (0, 512, 512), "y12": (2, 512, 512), "y11a": (1, 512, 256), "y11b": (1, 768, 256)}
+SCORE_TILES = {
+    "y00": (0, 0, 512),
+    "y01": (1, 0, 512),
+    "y02": (2, 0, 512),
+    "y10": (0, 512, 512),
+    "y12": (2, 512, 512),
+    "y11a": (1, 512, 256),
+    "y11b": (1, 768, 256),
+}
 
-RING = {"bank": 8, "h_slots": 4, "y_slots": 5, "partner": 6, "y_rows": 8, "packedV": 3, "packedS": 2, "packedG": 1, "packedH": 1}
+RING = {
+    "bank": 8,
+    "h_slots": 4,
+    "y_slots": 5,
+    "partner": 6,
+    "y_rows": 8,
+    "packedV": 3,
+    "packedS": 2,
+    "packedG": 1,
+    "packedH": 1,
+}
 
 ORDER = """
 ls10 loadQ0 is10@S loadW loadQs loadP0 orderQ0 loadPs loadQ1 turnW ls00 loadP1 qs10 ls11 ls01
@@ -52,39 +72,40 @@ def tile_cubed_walk_seed_scores_h2_kernel(
         def kept(name, shape, dtype):
             return keep.tile(shape, dtype, name=name, align_bytes=64)
 
-        turns = {}
+        last_used = {}
 
         def ring(pool, name, shape, dtype):
-            turns[name] = (turns.get(name, -1) + 1) % RING[name]
-            return pool.tile(shape, dtype, name="%s%d" % (name, turns[name]), align_bytes=64 if pool is work else None)
+            last_used[name] = (last_used.get(name, -1) + 1) % RING[name]
+            return pool.tile(
+                shape, dtype, name="%s%d" % (name, last_used[name]), align_bytes=64 if pool is work else None
+            )
 
-        halves = range(NODE_GROUPS)
-        p_words = [kept("p_words%d" % h, [P, NODE_GROUPS, W], U32) for h in halves]
+        groups = range(NODE_GROUPS)
+        p_words = [kept("p_words%d" % h, [P, NODE_GROUPS, W], U32) for h in groups]
         p_scales = kept("p_scales", [P, NODE_GROUPS, D], U8)
-        q_raw = [kept("q_raw%d" % g, [P, NODE_GROUPS, 2 * W], U8) for g in halves]
+        q_raw = [kept("q_raw%d" % g, [P, NODE_GROUPS, FP4_BYTES * W], U8) for g in groups]
         q_scales_raw = kept("q_scales_raw", [P, NODE_GROUPS, D], U8)
-        q_words = [kept("q_words%d" % g, [P, NODE_GROUPS, 2 * W], U8) for g in halves]
-        q_scales = [kept("q_scales%d" % g, [P, NODE_GROUPS, W], U8) for g in halves]
+        q_words = [kept("q_words%d" % g, [P, NODE_GROUPS, FP4_BYTES * W], U8) for g in groups]
+        q_scales = [kept("q_scales%d" % g, [P, NODE_GROUPS, W], U8) for g in groups]
         weight_rows = kept("weight_rows", [P, NODE_GROUPS, P], BF16)
         weight = kept("weight", [P, NODE_GROUPS, PACK], F32)
         thr = kept("thr", [P, SEED_GROUPS, PACK], BF16)
         thr_bias = kept("thr_bias", [P, SEED_GROUPS, PACK], F32)
         ident_bf16 = kept("ident_bf16", [P, P], BF16)
         ident_f32 = kept("ident_f32", [P, P], F32)
-        warm = kept("warm", [P, 1], F32)
-        y_scales = [kept("y_scales%d" % h, [P, SEED_GROUPS, W], U8) for h in halves]
+        y_scales = [kept("y_scales%d" % h, [P, SEED_GROUPS, W], U8) for h in groups]
 
         slots = {}
         packed = {}
         codes = {}
         scales = {}
-        for g in halves:
+        for g in groups:
             for s in range(SEED_GROUPS):
                 name = "s%d%d" % (g, s)
                 slots[name] = kept("raw_" + name, [P, PACK, W], BF16)
                 codes[name] = kept("codes_" + name, [P, W], U32)[:]
                 scales[name] = kept("scales_" + name, [P, W], U8)[:]
-            for h in halves:
+            for h in groups:
                 name = "h%d%d" % (h, g)
                 codes[name] = kept("codes_" + name, [P, W], U32)[:]
                 scales[name] = kept("scales_" + name, [P, W], U8)[:]
@@ -92,28 +113,28 @@ def tile_cubed_walk_seed_scores_h2_kernel(
             codes[name] = kept("codes_" + name, [P, width], U32)[:]
             scales[name] = y_scales[m0 // W][:, s, m0 % W : m0 % W + width]
 
-        nc.vector.memset(warm[:], 0.0)
-        nc.scalar.activation(out=warm[:], in_=warm[:], func=ACT.Square)
+        nc.vector.memset(ident_bf16[:], 0.0)
+        make_identity(nc, ident_bf16[:], nomemset=True)
+        nc.scalar.activation(out=ident_f32[:], in_=ident_bf16[:], func=ACT.Square)
         nc.vector.memset(q_scales_raw[:].rearrange("p c n -> p (c n)").bitcast(I32), 0)
         nc.vector.memset(p_scales[:].rearrange("p c n -> p (c n)").bitcast(I32), 0)
         nc.vector.memset(weight_rows[:], 0.0)
-        for ident in (ident_bf16, ident_f32):
-            nc.vector.memset(ident[:], 0.0)
-            make_identity(nc, ident[:], nomemset=True)
 
         def load_p(h):
             src = left_words.rearrange("c p n t -> p c (n t)")[:, :, h * W * PACK : (h + 1) * W * PACK]
             nc.sync.dma_start(out=p_words[h][:].bitcast(I32), in_=src.bitcast(I32))
 
         def load_q(g):
-            src = right_words.rearrange("c p n -> p c n")[:, :, g * 2 * W : (g + 1) * 2 * W]
+            src = right_words.rearrange("c p n -> p c n")[:, :, g * FP4_BYTES * W : (g + 1) * FP4_BYTES * W]
             nc.sync.dma_start(out=q_raw[g][:].bitcast(I32), in_=src.bitcast(I32))
 
-        def load_scales(plane, src):
+        def load_scales(tile, src):
             rows = src.rearrange("c r n -> r c n")
             for q in range(P // QUADRANT):
-                live = plane[QUADRANT * q : QUADRANT * q + 4]
-                nc.sync.dma_start(out=live.bitcast(I32), in_=rows[4 * q : 4 * q + 4].bitcast(I32))
+                live = tile[QUADRANT * q : QUADRANT * q + SCALE_ROWS]
+                nc.sync.dma_start(
+                    out=live.bitcast(I32), in_=rows[SCALE_ROWS * q : SCALE_ROWS * (q + 1)].bitcast(I32)
+                )
 
         def load_seeds(g, s):
             rows = seeds[g * W : (g + 1) * W, s * W : (s + 1) * W].rearrange("(b t r) n -> t b r n", t=PACK, r=RUN)
@@ -129,7 +150,7 @@ def tile_cubed_walk_seed_scores_h2_kernel(
 
         def reorder_q(g):
             for dst, src, run in (
-                (q_words[g][:], q_raw[g][:], RUN // 2),
+                (q_words[g][:], q_raw[g][:], RUN * FP4_BYTES // 4),
                 (q_scales[g][:], q_scales_raw[:, :, g * W : (g + 1) * W], RUN // 4),
             ):
                 nc.vector.tensor_copy(
@@ -139,7 +160,7 @@ def tile_cubed_walk_seed_scores_h2_kernel(
 
         def turn_weight():
             bank = ring(psum, "bank", [P, NODE_GROUPS, P], BF16)
-            for g in halves:
+            for g in groups:
                 nc.tensor.transpose(bank[:, g, :], weight_rows[:, g, :], ident_bf16[:])
             nc.scalar.copy(out=weight[:], in_=bank[:, :, :PACK])
 
@@ -148,16 +169,16 @@ def tile_cubed_walk_seed_scores_h2_kernel(
 
         def product(width, operands):
             bank = ring(psum, "bank", [P, width], F32)
-            for c in halves:
-                lhsT, lhsT_scale, rhs, rhs_scale = operands(c)
+            for group in groups:
+                lhsT, lhsT_scale, rhs, rhs_scale = operands(group)
                 nc.tensor.matmul_mx(
                     out=bank[:],
                     lhsT=lhsT,
                     lhsT_scale=lhsT_scale,
                     rhs=rhs,
                     rhs_scale=rhs_scale,
-                    start=(c == 0),
-                    stop=(c == NODE_GROUPS - 1),
+                    start=(group == 0),
+                    stop=(group == NODE_GROUPS - 1),
                 )
             return bank
 
@@ -169,7 +190,7 @@ def tile_cubed_walk_seed_scores_h2_kernel(
                 bank = product(
                     W,
                     lambda c: (
-                        q_words[g][:, c, t * 2 * P : (t + 1) * 2 * P].bitcast(FP4X4),
+                        q_words[g][:, c, t * FP4_BYTES * P : (t + 1) * FP4_BYTES * P].bitcast(FP4X4),
                         q_scales[g][:, c, t * P : (t + 1) * P],
                         p_words[h][:, c, :].bitcast(FP8X4),
                         p_scales[:, c, h * W : (h + 1) * W],
@@ -215,24 +236,18 @@ def tile_cubed_walk_seed_scores_h2_kernel(
                 )
 
         def interleave(name, engine):
-            on_gpsimd = engine in "GH"
             width = slots[name].shape[2]
             tile = ring(work, "packed" + engine, [P, width, PACK], BF16)
             packed[name] = tile
-            if name[0] == "s":
-                walk = "p m t i"
-                dst = tile[:].rearrange("p (i m) t -> " + walk, i=PACK)
-                src = slots[name][:].rearrange("p t (m i) -> " + walk, i=PACK)
-            else:
-                walk = "p m t i"
-                dst = tile[:].rearrange("p (m i) t -> " + walk, i=PACK)
-                src = slots[name][:].rearrange("p t (m i) -> " + walk, i=PACK)
-            if on_gpsimd:
-                nc.gpsimd.tensor_scalar(out=dst, in0=src, scalar1=1.0, scalar2=1.0, op0=ALU.mult, op1=ALU.mult)
-            elif engine == "S":
+            columns = "(i m)" if name[0] == "s" else "(m i)"
+            dst = tile[:].rearrange("p %s t -> p m t i" % columns, i=PACK)
+            src = slots[name][:].rearrange("p t (m i) -> p m t i", i=PACK)
+            if engine == "S":
                 nc.scalar.copy(out=dst, in_=src)
-            else:
+            elif engine == "V":
                 nc.vector.tensor_copy(out=dst, in_=src)
+            else:
+                nc.gpsimd.tensor_scalar(out=dst, in0=src, scalar1=1.0, scalar2=1.0, op0=ALU.mult, op1=ALU.mult)
 
         def quantize(name):
             nc.vector.quantize_mx(
@@ -246,43 +261,26 @@ def tile_cubed_walk_seed_scores_h2_kernel(
         def store_scales(h):
             rows = out_2.rearrange("s r m -> r s m")[:, :, h * W : (h + 1) * W]
             for q in range(P // QUADRANT):
-                live = y_scales[h][QUADRANT * q : QUADRANT * q + 4]
-                nc.sync.dma_start(out=rows[4 * q : 4 * q + 4].bitcast(I32), in_=live.bitcast(I32))
+                live = y_scales[h][QUADRANT * q : QUADRANT * q + SCALE_ROWS]
+                nc.sync.dma_start(
+                    out=rows[SCALE_ROWS * q : SCALE_ROWS * (q + 1)].bitcast(I32), in_=live.bitcast(I32)
+                )
 
         def turn(name, first, engines):
-            s, m0, width = SCORE_TILES[name]
+            s, m0 = SCORE_TILES[name][:2]
             for j, engine in zip((first, first + 1), engines):
                 bank = ring(psum, "bank", [P, PACK, P], F32)
                 for t in range(PACK):
                     nc.tensor.transpose(bank[:, t, :], slots[name][:, t, j * P : (j + 1) * P], ident_f32[:])
-                y = ring(work, "y_rows", [P, W], F32)
-                dst = y[:].rearrange("m (p t) -> m p t", t=PACK)
+                y_rows = ring(work, "y_rows", [P, W], F32)
+                dst = y_rows[:].rearrange("m (p t) -> m p t", t=PACK)
                 src = bank[:].rearrange("m t p -> m p t")
                 if engine == "S":
                     nc.scalar.copy(out=dst, in_=src)
                 else:
                     nc.vector.tensor_copy(out=dst, in_=src)
                 row = m0 + j * P
-                nc.sync.dma_start(out=out_0[row : row + P, s * W : (s + 1) * W], in_=y[:])
-
-        def run(step):
-            word, engines = (step + "@").split("@")[:2]
-            verb, name = word[0], word[1:].replace("+", "")
-            first = 2 if "+" in word else 0
-            if step in single:
-                single[step]()
-            elif verb == "l":
-                load_seeds(int(name[1]), int(name[2]))
-            elif verb == "m" and name[0] == "h":
-                cube(int(name[1]), int(name[2]), first)
-            elif verb == "m":
-                score(name, first)
-            elif verb == "i":
-                interleave(name, engines)
-            elif verb == "q":
-                quantize(name)
-            else:
-                turn(name, first, engines)
+                nc.sync.dma_start(out=out_0[row : row + P, s * W : (s + 1) * W], in_=y_rows[:])
 
         single = {
             "loadP0": lambda: load_p(0),
@@ -300,5 +298,22 @@ def tile_cubed_walk_seed_scores_h2_kernel(
             "storeS0": lambda: store_scales(0),
             "storeS1": lambda: store_scales(1),
         }
+
         for step in ORDER.split():
-            run(step)
+            text, engines = (step + "@").split("@")[:2]
+            verb, name = text[0], text[1:].replace("+", "")
+            first = 2 if "+" in text else 0
+            if step in single:
+                single[step]()
+            elif verb == "l":
+                load_seeds(int(name[1]), int(name[2]))
+            elif verb == "m" and name[0] == "h":
+                cube(int(name[1]), int(name[2]), first)
+            elif verb == "m":
+                score(name, first)
+            elif verb == "i":
+                interleave(name, engines)
+            elif verb == "q":
+                quantize(name)
+            else:
+                turn(name, first, engines)

from contextlib import ExitStack

import concourse.mybir as mybir
from concourse.masks import make_identity

D, S = 1024, 1536
SLOPE = 0.25
FLOPS = 2 * D * D * D + 2 * D * D * S

F32 = mybir.dt.float32
BF16 = mybir.dt.bfloat16
I32 = mybir.dt.int32
U32 = mybir.dt.uint32
U8 = mybir.dt.uint8
FP8X4 = mybir.dt.float8_e4m3fn_x4
FP4X4 = mybir.dt.float4_e2m1fn_x4
ALU = mybir.AluOpType
ACT = mybir.ActivationFunctionType

P = 128
PACK = 4
RUN = 8
W = P * PACK
FP4_BYTES = 2
QUADRANT = 32
SCALE_ROWS = QUADRANT // RUN
NODE_GROUPS = D // W
SEED_GROUPS = S // W

SCORE_TILES = {
    "y00": (0, 0, 512),
    "y01": (1, 0, 512),
    "y02": (2, 0, 512),
    "y10": (0, 512, 512),
    "y12": (2, 512, 512),
    "y11a": (1, 512, 256),
    "y11b": (1, 768, 256),
}

RING = {
    "bank": 8,
    "h_slots": 4,
    "y_slots": 5,
    "partner": 6,
    "y_rows": 8,
    "packedV": 3,
    "packedS": 2,
    "packedG": 1,
    "packedH": 1,
}

ORDER = """
ls10 loadQ0 is10@S loadW loadQs loadP0 orderQ0 loadPs loadQ1 turnW ls00 loadP1 qs10 ls11 ls01
orderQ1 mh00 mh00+ mh01 mh01+ mh10 mh11 is01@V loadT ih00@V ih01@S is00@H qs01 scaleT ls12 qh00 qh01
qs00 is11@G ls02 is02@S is12@H qs11 mh11+ mh10+ my01 qs12 ih11@H qs02 my01+ my00 my00+ my02 ih10@G
ty01@SS my02+ ty01+@SS qh11 ty00+@SS qh10 ty00@SV ty02@VS ty02+@VV iy01@H iy00@G my10 my10+ my12
ty10@SS qy01 qy00 my12+ ty10+@SV my11a ty12@SV ty12+@SV iy02@H my11a+ my11b my11b+ ty11a@SV iy10@S
iy12@G qy02 qy12 iy11a@H storeS0 ty11b@VV qy10 iy11b@S qy11a qy11b storeS1
"""


def tile_cubed_walk_seed_scores_h2_kernel(
    tc, left_words, left_scales, right_words, right_scales, node_weight, seeds, threshold, out_0, out_1, out_2
):
    nc = tc.nc
    with ExitStack() as ctx:
        keep = ctx.enter_context(tc.tile_pool(name="keep", bufs=1))
        work = ctx.enter_context(tc.tile_pool(name="work", bufs=1))
        psum = ctx.enter_context(tc.psum_pool(name="psum", bufs=1))
        ctx.enter_context(tc.manual_schedule())

        def kept(name, shape, dtype):
            return keep.tile(shape, dtype, name=name, align_bytes=64)

        last_used = {}

        def ring(pool, name, shape, dtype):
            last_used[name] = (last_used.get(name, -1) + 1) % RING[name]
            return pool.tile(
                shape, dtype, name="%s%d" % (name, last_used[name]), align_bytes=64 if pool is work else None
            )

        groups = range(NODE_GROUPS)
        p_words = [kept("p_words%d" % h, [P, NODE_GROUPS, W], U32) for h in groups]
        p_scales = kept("p_scales", [P, NODE_GROUPS, D], U8)
        q_raw = [kept("q_raw%d" % g, [P, NODE_GROUPS, FP4_BYTES * W], U8) for g in groups]
        q_scales_raw = kept("q_scales_raw", [P, NODE_GROUPS, D], U8)
        q_words = [kept("q_words%d" % g, [P, NODE_GROUPS, FP4_BYTES * W], U8) for g in groups]
        q_scales = [kept("q_scales%d" % g, [P, NODE_GROUPS, W], U8) for g in groups]
        weight_rows = kept("weight_rows", [P, NODE_GROUPS, P], BF16)
        weight = kept("weight", [P, NODE_GROUPS, PACK], F32)
        thr = kept("thr", [P, SEED_GROUPS, PACK], BF16)
        thr_bias = kept("thr_bias", [P, SEED_GROUPS, PACK], F32)
        ident_bf16 = kept("ident_bf16", [P, P], BF16)
        ident_f32 = kept("ident_f32", [P, P], F32)
        y_scales = [kept("y_scales%d" % h, [P, SEED_GROUPS, W], U8) for h in groups]

        slots = {}
        packed = {}
        codes = {}
        scales = {}
        for g in groups:
            for s in range(SEED_GROUPS):
                name = "s%d%d" % (g, s)
                slots[name] = kept("raw_" + name, [P, PACK, W], BF16)
                codes[name] = kept("codes_" + name, [P, W], U32)[:]
                scales[name] = kept("scales_" + name, [P, W], U8)[:]
            for h in groups:
                name = "h%d%d" % (h, g)
                codes[name] = kept("codes_" + name, [P, W], U32)[:]
                scales[name] = kept("scales_" + name, [P, W], U8)[:]
        for name, (s, m0, width) in SCORE_TILES.items():
            codes[name] = kept("codes_" + name, [P, width], U32)[:]
            scales[name] = y_scales[m0 // W][:, s, m0 % W : m0 % W + width]

        nc.vector.memset(ident_bf16[:], 0.0)
        make_identity(nc, ident_bf16[:], nomemset=True)
        nc.scalar.activation(out=ident_f32[:], in_=ident_bf16[:], func=ACT.Square)
        nc.vector.memset(q_scales_raw[:].rearrange("p c n -> p (c n)").bitcast(I32), 0)
        nc.vector.memset(p_scales[:].rearrange("p c n -> p (c n)").bitcast(I32), 0)
        nc.vector.memset(weight_rows[:], 0.0)

        def load_p(h):
            src = left_words.rearrange("c p n t -> p c (n t)")[:, :, h * W * PACK : (h + 1) * W * PACK]
            nc.sync.dma_start(out=p_words[h][:].bitcast(I32), in_=src.bitcast(I32))

        def load_q(g):
            src = right_words.rearrange("c p n -> p c n")[:, :, g * FP4_BYTES * W : (g + 1) * FP4_BYTES * W]
            nc.sync.dma_start(out=q_raw[g][:].bitcast(I32), in_=src.bitcast(I32))

        def load_scales(tile, src):
            rows = src.rearrange("c r n -> r c n")
            for q in range(P // QUADRANT):
                live = tile[QUADRANT * q : QUADRANT * q + SCALE_ROWS]
                nc.sync.dma_start(
                    out=live.bitcast(I32), in_=rows[SCALE_ROWS * q : SCALE_ROWS * (q + 1)].bitcast(I32)
                )

        def load_seeds(g, s):
            rows = seeds[g * W : (g + 1) * W, s * W : (s + 1) * W].rearrange("(b t r) n -> t b r n", t=PACK, r=RUN)
            for t in range(PACK):
                nc.sync.dma_start(out=slots["s%d%d" % (g, s)][:, t, :], in_=rows[t])

        def load_weight():
            src = node_weight.rearrange("(b t r) -> t b r", t=PACK, r=RUN)
            nc.sync.dma_start(out=weight_rows[:PACK].rearrange("t g (b r) -> t (g b) r", r=RUN), in_=src)

        def load_threshold():
            nc.sync.dma_start(out=thr[:], in_=threshold.rearrange("(s p t) -> p s t", p=P, t=PACK))

        def reorder_q(g):
            for dst, src, run in (
                (q_words[g][:], q_raw[g][:], RUN * FP4_BYTES // 4),
                (q_scales[g][:], q_scales_raw[:, :, g * W : (g + 1) * W], RUN // 4),
            ):
                nc.vector.tensor_copy(
                    out=dst.bitcast(I32).rearrange("p c (t b r) -> p c t b r", t=PACK, r=run),
                    in_=src.bitcast(I32).rearrange("p c (b t r) -> p c t b r", t=PACK, r=run),
                )

        def turn_weight():
            bank = ring(psum, "bank", [P, NODE_GROUPS, P], BF16)
            for g in groups:
                nc.tensor.transpose(bank[:, g, :], weight_rows[:, g, :], ident_bf16[:])
            nc.scalar.copy(out=weight[:], in_=bank[:, :, :PACK])

        def scale_threshold():
            nc.scalar.activation(out=thr_bias[:], in_=thr[:], func=ACT.Copy, scale=-SLOPE)

        def product(width, operands):
            bank = ring(psum, "bank", [P, width], F32)
            for group in groups:
                lhsT, lhsT_scale, rhs, rhs_scale = operands(group)
                nc.tensor.matmul_mx(
                    out=bank[:],
                    lhsT=lhsT,
                    lhsT_scale=lhsT_scale,
                    rhs=rhs,
                    rhs_scale=rhs_scale,
                    start=(group == 0),
                    stop=(group == NODE_GROUPS - 1),
                )
            return bank

        def cube(h, g, first):
            name = "h%d%d" % (h, g)
            if first == 0:
                slots[name] = ring(work, "h_slots", [P, PACK, W], BF16)
            for t in (first, first + 1):
                bank = product(
                    W,
                    lambda c: (
                        q_words[g][:, c, t * FP4_BYTES * P : (t + 1) * FP4_BYTES * P].bitcast(FP4X4),
                        q_scales[g][:, c, t * P : (t + 1) * P],
                        p_words[h][:, c, :].bitcast(FP8X4),
                        p_scales[:, c, h * W : (h + 1) * W],
                    ),
                )
                square = ring(work, "partner", [P, W], F32)
                nc.scalar.activation(out=square[:], in_=bank[:], func=ACT.Square)
                nc.vector.scalar_tensor_tensor(
                    out=slots[name][:, t, :],
                    in0=bank[:],
                    scalar=weight[:, g, t : t + 1],
                    in1=square[:],
                    op0=ALU.mult,
                    op1=ALU.mult,
                )

        def score(name, first):
            s, m0, width = SCORE_TILES[name]
            h, cols = m0 // W, slice(m0 % W, m0 % W + width)
            if first == 0:
                slots[name] = ring(work, "y_slots", [P, PACK, width], F32)
            for t in (first, first + 1):
                bank = product(
                    width,
                    lambda g: (
                        codes["s%d%d" % (g, s)][:, t * P : (t + 1) * P].bitcast(FP8X4),
                        scales["s%d%d" % (g, s)][:, t * P : (t + 1) * P],
                        codes["h%d%d" % (h, g)][:, cols].bitcast(FP8X4),
                        scales["h%d%d" % (h, g)][:, cols],
                    ),
                )
                sloped = ring(work, "partner", [P, width], F32)
                nc.scalar.activation(
                    out=sloped[:], in_=bank[:], func=ACT.Identity, scale=SLOPE, bias=thr_bias[:, s, t : t + 1]
                )
                nc.vector.scalar_tensor_tensor(
                    out=slots[name][:, t, :],
                    in0=bank[:],
                    scalar=thr[:, s, t : t + 1],
                    in1=sloped[:],
                    op0=ALU.subtract,
                    op1=ALU.max,
                )

        def interleave(name, engine):
            width = slots[name].shape[2]
            tile = ring(work, "packed" + engine, [P, width, PACK], BF16)
            packed[name] = tile
            columns = "(i m)" if name[0] == "s" else "(m i)"
            dst = tile[:].rearrange("p %s t -> p m t i" % columns, i=PACK)
            src = slots[name][:].rearrange("p t (m i) -> p m t i", i=PACK)
            if engine == "S":
                nc.scalar.copy(out=dst, in_=src)
            elif engine == "V":
                nc.vector.tensor_copy(out=dst, in_=src)
            else:
                nc.gpsimd.tensor_scalar(out=dst, in0=src, scalar1=1.0, scalar2=1.0, op0=ALU.mult, op1=ALU.mult)

        def quantize(name):
            nc.vector.quantize_mx(
                out=codes[name].bitcast(FP8X4), scales=scales[name], in_=packed[name][:].rearrange("p m t -> p (m t)")
            )
            if name in SCORE_TILES:
                s, m0, width = SCORE_TILES[name]
                dst = out_1[s].rearrange("p m t -> p (m t)")[:, m0 * PACK : (m0 + width) * PACK]
                nc.sync.dma_start(out=dst.bitcast(I32), in_=codes[name].bitcast(I32))

        def store_scales(h):
            rows = out_2.rearrange("s r m -> r s m")[:, :, h * W : (h + 1) * W]
            for q in range(P // QUADRANT):
                live = y_scales[h][QUADRANT * q : QUADRANT * q + SCALE_ROWS]
                nc.sync.dma_start(
                    out=rows[SCALE_ROWS * q : SCALE_ROWS * (q + 1)].bitcast(I32), in_=live.bitcast(I32)
                )

        def turn(name, first, engines):
            s, m0 = SCORE_TILES[name][:2]
            for j, engine in zip((first, first + 1), engines):
                bank = ring(psum, "bank", [P, PACK, P], F32)
                for t in range(PACK):
                    nc.tensor.transpose(bank[:, t, :], slots[name][:, t, j * P : (j + 1) * P], ident_f32[:])
                y_rows = ring(work, "y_rows", [P, W], F32)
                dst = y_rows[:].rearrange("m (p t) -> m p t", t=PACK)
                src = bank[:].rearrange("m t p -> m p t")
                if engine == "S":
                    nc.scalar.copy(out=dst, in_=src)
                else:
                    nc.vector.tensor_copy(out=dst, in_=src)
                row = m0 + j * P
                nc.sync.dma_start(out=out_0[row : row + P, s * W : (s + 1) * W], in_=y_rows[:])

        single = {
            "loadP0": lambda: load_p(0),
            "loadP1": lambda: load_p(1),
            "loadQ0": lambda: load_q(0),
            "loadQ1": lambda: load_q(1),
            "loadPs": lambda: load_scales(p_scales, left_scales),
            "loadQs": lambda: load_scales(q_scales_raw, right_scales),
            "loadW": load_weight,
            "loadT": load_threshold,
            "orderQ0": lambda: reorder_q(0),
            "orderQ1": lambda: reorder_q(1),
            "turnW": turn_weight,
            "scaleT": scale_threshold,
            "storeS0": lambda: store_scales(0),
            "storeS1": lambda: store_scales(1),
        }

        for step in ORDER.split():
            text, engines = (step + "@").split("@")[:2]
            verb, name = text[0], text[1:].replace("+", "")
            first = 2 if "+" in text else 0
            if step in single:
                single[step]()
            elif verb == "l":
                load_seeds(int(name[1]), int(name[2]))
            elif verb == "m" and name[0] == "h":
                cube(int(name[1]), int(name[2]), first)
            elif verb == "m":
                score(name, first)
            elif verb == "i":
                interleave(name, engines)
            elif verb == "q":
                quantize(name)
            else:
                turn(name, first, engines)
